import numpy as np, ml_dtypes
CORES = [51,54,179,182]
N = 4
BF = ml_dtypes.bfloat16
S, M = 3072, 1024
def pack(x, slot, w):
    return {"x": np.clip(np.rint(x), -255, 255).astype(np.int32).astype(np.float32).astype(BF), "slot": slot.astype(np.int32), "w": np.rint(w).astype(np.int32).astype(np.float32)}
def setup_inputs(rng):
    x = rng.standard_normal((N, 128, S), dtype=np.float32) * rng.integers(20, 61, (1, 128, 1)) + rng.integers(-80, 81, (1, 128, 1)) + rng.integers(-15, 16, (N, 128, 1))
    slot = np.floor(M * rng.random((N, 8, S)) ** rng.integers(1, 4, (1, 8, 1))).astype(np.int64) ^ rng.integers(0, M, (1, 8, 1))
    return pack(x, slot, rng.integers(-255, 256, (N, 128, 1)))
def setup_inputs_one(rng):
    d = setup_inputs(rng); e = rng.integers(0, M, (1, 8, 1)); e[0, 0] = 0; e[0, 7] = M - 1
    d["slot"][:] = e; d["w"].reshape(N, 8, 16)[:, ::2] = 0; return d
def setup_inputs_gaps(rng):
    x = np.floor(255 * rng.random((N, 128, S)) ** 4) - 255
    slot = 2 * rng.integers(0, M // 2, (N, 8, S)) + ((np.arange(N)[:, None, None] + np.arange(8)[:, None]) & 1)
    z = rng.integers(0, M, (1, 8, 1)); slot = np.where(slot == z, slot ^ 2, slot)
    slot[0, :, S - 1] = z[0, :, 0]; slot[N - 1, :, 0] = z[0, :, 0]
    x[0, :, S - 1] = rng.integers(-60, 0, 128); x[N - 1, :, 0] = -255
    return pack(x, slot, rng.integers(-255, 256, (N, 128, 1)))
def setup_inputs_ends(rng):
    p = rng.choice(np.array([0, 2.0 ** -6, 2.0 ** -11]), 128); p[0] = 0; p[1] = 2.0 ** -6
    x = np.where(rng.random((N, 128, S)) < p[:, None], 255, -255)
    slot = rng.integers(0, M, (N, 8, S)); slot[:, 1::2] = rng.choice(np.array([0, 1, M - 2, M - 1]), (N, 4, S))
    w = rng.choice(np.array([-255, 255]), (N, 128, 1)); w[:, :16] = 255
    return pack(x, slot, w)
def setup_inputs_spread(rng):
    x = rng.integers(-255, 256, (N, 128, S)) * np.exp2(-rng.integers(0, 9, (N, 1, S)))
    slot = np.floor(M * rng.random((N, 8, S)) ** rng.integers(1, 13, (N, 8, 1))).astype(np.int64) ^ rng.integers(0, M, (1, 8, 1))
    return pack(x, slot, rng.integers(-255, 256, (N, 128, 1)) * np.exp2(-rng.integers(0, 8, (N, 128, 1))))
def check_inputs(d):
    bad = []
    for k in ("x", "w"):
        v = d[k].astype(np.float32)
        if not (np.all(np.abs(v) <= 255) and np.all(v == np.rint(v))): bad.append(k + " whole, -255 to 255")
    if not (np.all(d["slot"] >= 0) and np.all(d["slot"] < M)): bad.append("slot 0 to M - 1")
    return bad
def reference(x, slot, w):
    h = np.arange(8)
    v = np.ascontiguousarray(x.astype(np.float32).astype(np.int64).reshape(N, 8, 16, S).transpose(0, 3, 1, 2)).reshape(N * S, 8, 16)
    s = slot.transpose(0, 2, 1).reshape(N * S, 8)
    c = w.astype(np.int64).reshape(N, 1, 8, 16)
    for layer in range(2):
        if layer == 1: s = np.sum(v.reshape(N, S, 8, 16) * c, axis=3).reshape(N * S, 8) & (M - 1)
        m = np.full((8, M, 16), -256, np.int64); y = np.empty_like(v)
        for t in range(N * S):
            y[t] = np.maximum(m[h, s[t]], v[t]); m[h, s[t]] = y[t]
        v = y
    return {"y": np.ascontiguousarray(v.reshape(N, S, 8, 16).transpose(0, 2, 3, 1)).reshape(N, 128, S).astype(np.float32).astype(BF)}

@@ -1,0 +1,382 @@
+from concourse.bass import DstId, RemoteDMATransfer
+from concourse.mybir import dt, AluOpType, AxisListType, ActivationFunctionType
+
+S_TOK, NC, ND = 3072, 192, 32
+F = NC * ND
+GRP = 8 * NC
+HI = 24576
+NEG = -1000000.0
+
+SCRATCH = {
+    "sl_i": ("sbuf", [16, 1536], "int32"), "sl_h": ("sbuf", [16, 1536], "float16"),
+    "xs": ("sbuf", [128, S_TOK], "bfloat16"), "y1": ("sbuf", [128, S_TOK], "bfloat16"),
+    "yl": ("sbuf", [128, S_TOK], "bfloat16"), "yo": ("sbuf", [128, S_TOK], "bfloat16"),
+    "wc": ("sbuf", [128, 1], "float32"),
+    "ones": ("sbuf", [128, 288], "bfloat16"), "wd": ("sbuf", [16, 288], "bfloat16"),
+    "ident": ("sbuf", [128, 128], "bfloat16"), "bm": ("sbuf", [128, 128], "bfloat16"), "bt": ("sbuf", [128, 128], "bfloat16"),
+    "lm": ("sbuf", [128, 128], "bfloat16"), "um": ("sbuf", [128, 128], "bfloat16"),
+    "m2": ("sbuf", [128, 2048], "bfloat16"), "m3": ("sbuf", [128, 2048], "bfloat16"), "wm": ("sbuf", [128, 2048], "bfloat16"),
+    "pi": ("sbuf", [128, 1], "int32"), "li": ("sbuf", [128, 1], "int32"), "lane": ("sbuf", [128, 1], "float32"),
+    "ml": ("sbuf", [128, 32], "float32"), "dq": ("sbuf", [128, 32], "float32"), "hi192": ("sbuf", [128, 32], "float32"),
+    "kc": ("sbuf", [128, 1024], "float32"), "zero": ("sbuf", [128, GRP], "bfloat16"),
+    "ki": ("sbuf", [128, NC], "int32"), "loi": ("sbuf", [128, NC], "int32"), "hii": ("sbuf", [128, NC], "int32"),
+    "keyi": ("sbuf", [128, NC], "int32"), "h16": ("sbuf", [128, NC], "float32"), "pk": ("sbuf", [128, NC], "float16"),
+    "dig1": ("sbuf", [128, NC], "bfloat16"), "dig2": ("sbuf", [128, NC], "bfloat16"), "koff": ("sbuf", [128, NC], "uint16"),
+    "off1": ("sbuf", [128, NC], "uint16"), "off2": ("sbuf", [128, NC], "uint16"),
+    "eoff": ("sbuf", [128, 64], "uint16"), "lst": ("sbuf", [128, 64], "uint16"),
+    "oh": ("sbuf", [128, F + 16], "bfloat16"), "ct": ("sbuf", [128, F + 16], "bfloat16"), "msk": ("sbuf", [128, F], "float16"),
+    "ji": ("sbuf", [128, 32], "int32"), "jq": ("sbuf", [128, 32], "int32"), "jc": ("sbuf", [128, 32], "int32"),
+    "jt": ("sbuf", [128, 32], "float32"), "cw": ("sbuf", [128, 2], "float32"), "mk": ("sbuf", [128, 1024], "bfloat16"),
+    "g1": ("sbuf", [128, 1024], "bfloat16"), "g2": ("sbuf", [128, 1024], "bfloat16"),
+    "packed": ("sbuf", [128, S_TOK], "float32"), "krow": ("sbuf", [128, S_TOK], "float32"),
+    "los": ("sbuf", [128, S_TOK], "float32"), "ext": ("sbuf", [128, S_TOK], "bfloat16"),
+    "srt": ("sbuf", [128, S_TOK + 8], "float32"),
+    "tl0": ("sbuf", [128, 1024], "bfloat16"), "tl1": ("sbuf", [128, 1024], "bfloat16"),
+    "ld00": ("sbuf", [128, 1024], "bfloat16"), "ld01": ("sbuf", [128, 1024], "bfloat16"), "ld02": ("sbuf", [128, 1024], "bfloat16"),
+    "ld10": ("sbuf", [128, 1024], "bfloat16"), "ld11": ("sbuf", [128, 1024], "bfloat16"), "ld12": ("sbuf", [128, 1024], "bfloat16"),
+    "ta": ("sbuf", [128, 1024], "bfloat16"), "tb": ("sbuf", [128, 1024], "bfloat16"),
+    "psa": ("psum", [128, GRP], "float32"), "psb": ("psum", [128, GRP], "float32"),
+    "acc": ("psum", [128, 512], "float32"), "mis": ("psum", [128, 512], "float32"),
+}
+SEMAPHORES = (["cv", "cs", "cp", "cg", "dx0", "dx1", "ds0", "ds1", "dw", "dy0", "dy1", "lo0", "lo1"]
+              + ["r%d%d" % (a, b) for a in range(2) for b in range(3)])
+
+
+def mask_of(engines):
+    return sum(1 << e for e in engines)
+
+
+def rank_program(g, core, T, topo):
+    rank = T.rank_of(core)
+    if rank is None:
+        return
+    A, ACT = AluOpType, ActivationFunctionType
+    V, S, P, Y = g.vector, g.scalar, g.tensor, g.sync
+    queue = {"v": V, "s": S, "p": P, "g": g, "y": Y}
+    count = {"v": 0, "s": 0, "p": 0, "g": 0}
+    seen = {}
+    nranks = len(T.cores)
+    sends = rank < nranks - 1
+
+    def need(q, *toks):
+        best = {}
+        for t in toks:
+            if t is not None:
+                best[t[0]] = max(best.get(t[0], 0), t[1])
+        for s in sorted(best):
+            if seen.get((q, s), 0) < best[s]:
+                queue[q].wait_ge(T.sem[s], best[s])
+                seen[(q, s)] = best[s]
+
+    def done(q, ins):
+        count[q] += 1
+        ins.then_inc(T.sem["c" + q], 1)
+        return ("c" + q, count[q])
+
+    def dma(q, sem, out, in_, *deps):
+        need(q, *deps)
+        queue[q].dma_start(out, in_).then_inc(T.sem[sem], 16)
+        return (sem, 16)
+
+    def ts(out, in0, s1, s2, op0, op1, *deps):
+        need("v", *deps)
+        if op1 is None:
+            return done("v", V.tensor_scalar(out, in0, s1, None, op0))
+        return done("v", V.tensor_scalar(out, in0, s1, s2, op0, op1))
+
+    def tt(out, a, b, op, *deps):
+        need("v", *deps)
+        return done("v", V.tensor_tensor(out, a, b, op))
+
+    def vcopy(out, in_, *deps):
+        need("v", *deps)
+        return done("v", V.tensor_copy(out, in_))
+
+    def fill(ap, c):
+        return done("v", V.memset(ap, c))
+
+    def act(out, in_, *deps):
+        need("s", *deps)
+        return done("s", S.activation(out, in_, ACT.Copy))
+
+    def mm(out, lhsT, rhs, start, stop, *deps):
+        need("p", *deps)
+        return done("p", P.matmul(out, lhsT, rhs, start, stop))
+
+    t_s = [dma("y", "ds0", T.sl_i[0:8, :], T.slot[:, 0:1536]), dma("s", "ds1", T.sl_i[8:16, :], T.slot[:, 1536:3072])]
+    t_x = [dma("y", "dx0", T.xs[:, 0:1536], T.x[:, 0:1536]), dma("s", "dx1", T.xs[:, 1536:3072], T.x[:, 1536:3072])]
+    t_w = dma("y", "dw", T.wc[:], T.w[:])
+
+    f_one = fill(T.ones[:], 1.0)
+    f_m3 = fill(T.m3[:], 512.0)
+    fill(T.ct[:, 0:1], -128.0)
+    fill(T.ct[:, F + 1:F + 16], 0.0)
+    fill(T.oh[:, F:F + 16], 0.0)
+    fill(T.srt[:, 0:8], NEG)
+    f_zero = fill(T.zero[:], 0.0)
+    f_m2 = fill(T.m2[:], 1.0)
+
+    def sel(out, in_, pattern, op, base, cm, *deps):
+        need("g", *deps)
+        return done("g", g.affine_select(out, in_, pattern, op, 0.0, base, cm))
+
+    c_wd = sel(T.wd[:], T.ones[0:16, :], [[-1, 288]], A.is_equal, 15, 16, f_one)
+    t0 = sel(T.bt[:], T.ones[:, 0:128], [[-16, 8], [0, 16]], A.is_ge, 0, 1)
+    c_b = sel(T.bm[:], T.bt[:], [[16, 8], [0, 16]], A.is_ge, 15, -1, t0)
+    sel(T.lm[:], T.bm[:], [[1, 128]], A.is_gt, 0, -1, c_b)
+    c_lu = sel(T.um[:], T.bm[:], [[-1, 128]], A.is_ge, 0, 1)
+    c_id = sel(T.ident[:], T.ones[:, 0:128], [[-1, 128]], A.is_equal, 0, 1)
+    c_m3 = sel(T.m3[:], T.m3[:], [[-1, 16], [-16, 8], [0, 16]], A.is_equal, 0, 1, f_m3)
+    done("g", g.iota(T.pi[:], [[0, 1]], 0, 1))
+    done("g", g.iota(T.ml[:], [[0, 2], [1, 16]], 0, 0, allow_small_or_imprecise_dtypes=True))
+    c_io = done("g", g.iota(T.hi192[:], [[NC, 32]], 0, 0, allow_small_or_imprecise_dtypes=True))
+    t0 = sel(T.m2[:], T.m2[:], [[-1, 16], [0, 8], [1, 16]], A.is_equal, 0, 0, f_m2)
+    t0 = sel(T.m2[:], T.m2[:], [[0, 16], [-16, 8], [0, 16]], A.is_ge, 0, 1, t0)
+    c_m2 = sel(T.m2[:], T.m2[:], [[0, 16], [16, 8], [0, 16]], A.is_ge, 15, -1, t0)
+    c_kc = done("g", g.iota(T.kc[:], [[HI, 32], [512, 32]], 0, 0, allow_small_or_imprecise_dtypes=True))
+
+    t_k = None
+    v0 = vcopy(T.sl_h[:], T.sl_i[:], *t_s)
+    for h in range(2):
+        for q in range(16):
+            o = 128 * h + 15 - q
+            t_k = mm(T.mis[:, 96 * h:96 * h + 96], T.wd[:, o:o + 128], T.sl_h[:, q:1536:16], q == 0, q == 15, v0, c_wd)
+
+    st = {"lane": None, "wm": None}
+
+    def one_hot(dig, k, dep):
+        t = None
+        for d in range(8 * k, 8 * k + 8):
+            t = ts(T.oh[:, NC * d:NC * d + NC], dig, float(d), None, A.is_equal, None, dep)
+        need("v", t, f_zero)
+        a = GRP * k
+        init = -128.0 if k == 0 else T.ct[:, a:a + 1]
+        return done("v", V.tensor_tensor_scan(T.ct[:, a + 1:a + GRP + 1], T.oh[:, a:a + GRP], T.zero[:], init, A.add, A.add))
+
+    def sort_pass(dig, off, dep, ps_free, after_counts):
+        sc, ml = [None] * 4, [None] * 4
+        free = list(ps_free)
+        acc_t = [None]
+        ps = [T.psa, T.psb]
+
+        def counts(k):
+            sc[k] = one_hot(dig, k, dep if k == 0 else sc[k - 1])
+
+        def sums(k):
+            t = None
+            for b in range(3):
+                a = GRP * k + 512 * b
+                mm(ps[k % 2][:, 512 * b:512 * b + 512], T.lm[:], T.ct[:, a + 1:a + 513], True, False, sc[k], free[k % 2], c_lu)
+                t = mm(ps[k % 2][:, 512 * b:512 * b + 512], T.um[:], T.ct[:, a:a + 512], False, True)
+            return t
+
+        def pick(k, t):
+            a = GRP * k
+            ml[k] = tt(T.msk[:, a:a + GRP], ps[k % 2][:], T.oh[:, a:a + GRP], A.mult, t)
+            free[k % 2] = ml[k]
+
+        def reduce_(k):
+            for d in range(8 * k, 8 * k + 8):
+                acc_t[0] = mm(T.acc[:, 0:NC], T.ident[:], T.msk[:, NC * d:NC * d + NC], d == 0, d == ND - 1, ml[k], c_id)
+
+        counts(0)
+        u0 = sums(0)
+        counts(1)
+        u1 = sums(1)
+        pick(0, u0)
+        reduce_(0)
+        counts(2)
+        u2 = sums(2)
+        pick(1, u1)
+        reduce_(1)
+        counts(3)
+        u3 = sums(3)
+        if after_counts is not None:
+            after_counts(sc[3])
+        pick(2, u2)
+        reduce_(2)
+        pick(3, u3)
+        reduce_(3)
+        return ts(off[:], T.acc[:, 0:NC], 2048.0, None, A.add, None, acc_t[0]), sc[3], ml[3], free
+
+    def layer(li, src, src_toks, key_tok, out, half_done):
+        v = vcopy(T.ki[:], T.mis[:, 0:NC], key_tok)
+        v_lo = ts(T.loi[:], T.ki[:], 31, None, A.bitwise_and, None, v)
+        v_key = ts(T.keyi[:], T.ki[:], 1023, None, A.bitwise_and, None, v)
+        v_hi = ts(T.hii[:], T.ki[:], 1023, 5, A.bitwise_and, A.logical_shift_right, v)
+        v_d1 = vcopy(T.dig1[:], T.loi[:], v_lo)
+        v_h16 = ts(T.h16[:], T.hii[:], 16.0, None, A.mult, None, v_hi)
+        v_ko = vcopy(T.koff[:], T.keyi[:], v_key)
+        v_pk = tt(T.pk[:], T.keyi[:], T.h16[:], A.add, v_h16)
+        free = []
+        for h, ps in enumerate((T.psa, T.psb)):
+            t = None
+            for b in range(3):
+                c = 1536 * h + 512 * b
+                mm(ps[:, 512 * b:512 * b + 512], T.ident[:], src[:, c:c + 512], True, False, c_id, *src_toks)
+                for q in range(16):
+                    t = mm(ps[:, 512 * b + q:512 * b + 512:16], T.m3[:, 128 * q:128 * q + 128],
+                           T.pk[:, c // 16:c // 16 + 32], False, q == 15, v_pk, c_m3)
+            free.append(act(T.packed[:, 1536 * h:1536 * h + 1536], ps[:], t))
+        t_pk = free[1]
+
+        if st["lane"] is None:
+            v = ts(T.li[:], T.pi[:], 15, None, A.bitwise_and, None, c_io)
+            v = vcopy(T.lane[:], T.li[:], v)
+            st["lane"] = ts(T.dq[:], T.ml[:], T.lane[:], None, A.is_equal, None, v)
+
+        jt = [None]
+
+        def borders(tok):
+            if sends:
+                jt[0] = mm(T.mis[:, 0:32], T.bm[:], T.ct[:, NC:F + 1:NC], True, True, tok)
+
+        v_o1, _, v_m, free = sort_pass(T.dig1[:], T.off1, v_d1, free, borders)
+        t_kr = []
+        for h, ps in enumerate((T.psa, T.psb)):
+            t = None
+            for b in range(3):
+                for q in range(16):
+                    c = 1536 * h + 512 * b
+                    t = mm(ps[:, 512 * b + q:512 * b + 512:16], T.m3[:, 128 * q:128 * q + 128],
+                           T.pk[:, c // 16:c // 16 + 32], True, True, free[h])
+            t_kr.append(act(T.krow[:, 1536 * h:1536 * h + 1536], ps[:], t))
+        need("v", v_o1, t_pk)
+        v_s1 = done("v", V.tensor_copy(T.los[:].indirect(T.off1[:]), T.packed[:]))
+        t_hi, v_j = None, None
+        if sends:
+            v_j = ts(T.ji[:], T.mis[:, 0:32], 2048.0, None, A.add, None, jt[0])
+        for h in range(2):
+            need("s", v_s1)
+            t = done("s", S.activation(T.ext[:, 1536 * h:1536 * h + 1536], T.los[:, 1536 * h:1536 * h + 1536], ACT.Copy,
+                                       bias=-0.32 / 16.0, scale=1.0 / (16.0 * HI)))
+            for q in range(16):
+                t_hi = mm(T.mis[:, 96 * h:96 * h + 96], T.m2[:, 128 * q:128 * q + 128],
+                          T.ext[:, 1536 * h + q:1536 * h + 1536:16], q == 0, q == 15, t, c_m2, v_j)
+        if sends:
+            v_q = ts(T.jq[:], T.ji[:], 15, None, A.bitwise_and, None, v_j)
+            v_c = ts(T.jc[:], T.ji[:], 4, None, A.logical_shift_right, None, v_j)
+            v = tt(T.jt[:], T.jc[:], T.dq[:], A.mult, v_c, st["lane"])
+            v_mk = ts(T.mk[:, 0:32], T.jq[:], T.lane[:], None, A.is_gt, None, v_q)
+            need("v", v)
+            for b in range(2):
+                v = done("v", V.tensor_reduce(T.cw[:, b:b + 1], T.jt[:, 16 * b:16 * b + 16], AxisListType.X, A.add))
+            for b in range(2):
+                v_l = ts(T.lst[:, b:64:2], T.hi192[:], T.cw[:, b:b + 1], None, A.add, None, v, c_io)
+            s_mk, n = v_mk, 32
+            while n < 1024:
+                s_mk = act(T.mk[:, n:2 * n], T.mk[:, 0:n], s_mk)
+                n *= 2
+        if st["wm"] is None:
+            st["wm"] = ts(T.wm[:], T.m2[:], T.wc[:], None, A.mult, None, t_w, c_m2)
+        v = vcopy(T.hii[:], T.mis[:, 0:NC], t_hi)
+        v_d2 = vcopy(T.dig2[:], T.hii[:], v)
+
+        v_o2, v_sc, v_m, free = sort_pass(T.dig2[:], T.off2, v_d2, t_kr, None)
+        t_e = None
+        if sends:
+            need("s", v_sc, v_l)
+            s_g = done("s", S.activation(T.g1[:], T.ct[:].indirect(T.lst[:]), ACT.Copy))
+            v_g = tt(T.g2[:], T.oh[:].indirect(T.lst[:]), T.mk[:], A.mult, s_mk, v_l)
+            for q in range(16):
+                mm(T.mis[:, 0:64], T.m2[:, 128 * q:128 * q + 128], T.g1[:, q:1024:16], q == 0, False, s_g)
+            for q in range(16):
+                t_e = mm(T.mis[:, 0:64], T.m2[:, 128 * q:128 * q + 128], T.g2[:, q:1024:16], False, q == 15, v_g)
+        need("v", v_o2)
+        v = done("v", V.tensor_copy(T.packed[:].indirect(T.off2[:]), T.los[:]))
+        if sends:
+            v_e = ts(T.eoff[:], T.mis[:, 0:64], 2055.0, None, A.add, None, t_e)
+        need("v", v)
+        v_mx = done("v", V.tensor_tensor_scan(T.srt[:, 8:], T.packed[:], T.packed[:], NEG, A.max, A.max))
+        tl = T["tl%d" % li]
+        if sends:
+            v_t = tt(tl[:], T.srt[:].indirect(T.eoff[:]), T.kc[:], A.subtract, v_mx, v_e, c_kc)
+            need("g", v_t)
+            off_chip, on_chip = [], []
+            for d in T.cores[rank + 1:]:
+                (on_chip if d in topo.cores_of(core) else off_chip).append(d)
+            trans, total, used = [], 0, []
+            for group in (off_chip, on_chip):
+                if not group:
+                    continue
+                eng = [e for e in topo.engines(core, group[0]) if e not in used]
+                used += eng
+                total += len(eng)
+                dst = []
+                for d in group:
+                    rid, pid = topo.addr(d, core)
+                    dst.append(DstId(rid=rid, pnc=pid))
+                trans.append(RemoteDMATransfer(dst_ids=dst, dma_engine_mask=mask_of(eng), remote_sem=T.sem["r%d%d" % (li, rank)],
+                                               srcs=[tl[:]], dsts=[T["ld%d%d" % (li, rank)][:] for d in group]))
+            g.remote_dma_fused(trans, local_sem=T.sem["lo%d" % li])
+            st["lo%d" % li] = total
+        a = 64 if sends else 96
+        need("v", v_mx)
+        v_a = done("v", V.tensor_copy(T.los[:, 0:16 * a], T.srt[:, 8:].indirect(T.off2[:, 0:a])))
+        need("s", v_mx)
+        s_a = done("s", S.activation(T.los[:, 16 * a:], T.srt[:, 8:].indirect(T.off2[:, a:NC]), ACT.Copy))
+        tin, v_in = None, None
+        if rank > 0:
+            def landed(r):
+                d = T.cores[r]
+                n = 8
+                return ("r%d%d" % (li, r), arrivals(r))
+
+            def arrivals(r):
+                src_core = T.cores[r]
+                ups = T.cores[r + 1:]
+                offs = [d for d in ups if d not in topo.cores_of(src_core)]
+                if core in offs:
+                    return len(topo.engines(src_core, core))
+                taken = topo.engines(src_core, offs[0]) if offs else []
+                return len([e for e in topo.engines(src_core, core) if e not in taken])
+            tin = T["ld%d0" % li]
+            v_in = landed(0)
+            for r in range(1, rank):
+                ps = (T.psa, T.psb)[r % 2]
+                for b in range(2):
+                    t = mm(ps[:, 512 * b:512 * b + 512], T.ident[:], T["ld%d%d" % (li, r)][:, 512 * b:512 * b + 512], True, True,
+                           landed(r), v_m)
+                nxt = (T.ta, T.tb)[r % 2]
+                st["mx%d" % r] = (nxt, ps, t)
+        dst = T.yl if rank > 0 else out
+        ys = []
+        for h in range(2):
+            need("v", v_a, s_a, t_kr[1])
+            c = 1536 * h
+            ys.append(done("v", V.tensor_tensor(dst[:, c:c + 1536], T.los[:].indirect(T.off1[:, 96 * h:96 * h + 96]),
+                                                T.krow[:, c:c + 1536], A.subtract)))
+            if rank == 0:
+                half_done(h, ys[h])
+        if rank > 0:
+            for r in range(1, rank):
+                nxt, ps, t = st["mx%d" % r]
+                v_in = tt(nxt[:], ps[:, 0:1024], tin[:], A.max, t, v_in)
+                tin = nxt
+            for h in range(2):
+                c = 1536 * h
+                half_done(h, tt(out[:, c:c + 1536], tin[:].indirect(T.koff[:, 96 * h:96 * h + 96]), T.yl[:, c:c + 1536], A.max,
+                                v_in, ys[h], v_ko))
+
+    hk = {}
+
+    def hash_half(h, tok):
+        hk[h] = tok
+        for q in range(16):
+            hk["t"] = mm(T.mis[:, 96 * h:96 * h + 96], T.wm[:, 128 * q:128 * q + 128], T.y1[:, 1536 * h + q:1536 * h + 1536:16],
+                         q == 0, q == 15, tok, st["wm"])
+
+    def store_half(h, tok):
+        c = 1536 * h
+        dma("y", "dy%d" % h, T.y[:, c:c + 1536], T.yo[:, c:c + 1536], tok)
+
+    layer(0, T.xs, t_x, t_k, T.y1, hash_half)
+    layer(1, T.y1, [hk[0], hk[1]], hk["t"], T.yo, store_half)
+
+    for q in ("v", "s", "p", "g"):
+        need("g", ("c" + q, count[q]))
+    for s in ("ds0", "ds1", "dx0", "dx1", "dw", "dy0", "dy1"):
+        need("g", (s, 16))
+    if sends:
+        for li in range(2):
+            need("g", ("lo%d" % li, st["lo%d" % li]))

@@ -6,6 +6,8 @@ F = NC * ND
 GRP = 8 * NC
 HI = 24576
 NEG = -1000000.0
+ON_SCALAR = (2, 3)
+CUT = 1792
 
 SCRATCH = {
     "sl_i": ("sbuf", [16, 1536], "int32"), "sl_h": ("sbuf", [16, 1536], "float16"),
@@ -16,6 +18,7 @@ SCRATCH = {
     "ident": ("sbuf", [128, 128], "bfloat16"), "bm": ("sbuf", [128, 128], "bfloat16"), "bt": ("sbuf", [128, 128], "bfloat16"),
     "lm": ("sbuf", [128, 128], "bfloat16"), "um": ("sbuf", [128, 128], "bfloat16"),
     "m2": ("sbuf", [128, 2048], "bfloat16"), "m3": ("sbuf", [128, 2048], "bfloat16"), "wm": ("sbuf", [128, 2048], "bfloat16"),
+    "ms": ("sbuf", [128, 4096], "bfloat16"),
     "pi": ("sbuf", [128, 1], "int32"), "li": ("sbuf", [128, 1], "int32"), "lane": ("sbuf", [128, 1], "float32"),
     "ml": ("sbuf", [128, 32], "float32"), "dq": ("sbuf", [128, 32], "float32"), "hi192": ("sbuf", [128, 32], "float32"),
     "kc": ("sbuf", [128, 1024], "float32"), "zero": ("sbuf", [128, GRP], "bfloat16"),
@@ -25,8 +28,9 @@ SCRATCH = {
     "off1": ("sbuf", [128, NC], "uint16"), "off2": ("sbuf", [128, NC], "uint16"),
     "eoff": ("sbuf", [128, 64], "uint16"), "lst": ("sbuf", [128, 64], "uint16"),
     "oh": ("sbuf", [128, F + 16], "bfloat16"), "ct": ("sbuf", [128, F + 16], "bfloat16"), "msk": ("sbuf", [128, F], "float16"),
+    "ab0": ("sbuf", [128, GRP], "bfloat16"), "ab1": ("sbuf", [128, GRP], "bfloat16"),
     "ji": ("sbuf", [128, 32], "int32"), "jq": ("sbuf", [128, 32], "int32"), "jc": ("sbuf", [128, 32], "int32"),
-    "jt": ("sbuf", [128, 32], "float32"), "cw": ("sbuf", [128, 2], "float32"), "mk": ("sbuf", [128, 1024], "bfloat16"),
+    "jt": ("sbuf", [128, 32], "float32"), "cw": ("sbuf", [128, 2], "float32"), "mk": ("sbuf", [128, 32], "float32"),
     "g1": ("sbuf", [128, 1024], "bfloat16"), "g2": ("sbuf", [128, 1024], "bfloat16"),
     "packed": ("sbuf", [128, S_TOK], "float32"), "krow": ("sbuf", [128, S_TOK], "float32"),
     "los": ("sbuf", [128, S_TOK], "float32"), "ext": ("sbuf", [128, S_TOK], "bfloat16"),
@@ -99,6 +103,10 @@ def rank_program(g, core, T, topo):
         need("s", *deps)
         return done("s", S.activation(out, in_, ACT.Copy))
 
+    def act2(out, in_, func, bias, scale, *deps):
+        need("s", *deps)
+        return done("s", S.activation(out, in_, func, bias=bias, scale=scale))
+
     def mm(out, lhsT, rhs, start, stop, *deps):
         need("p", *deps)
         return done("p", P.matmul(out, lhsT, rhs, start, stop))
@@ -121,12 +129,12 @@ def rank_program(g, core, T, topo):
         return done("g", g.affine_select(out, in_, pattern, op, 0.0, base, cm))
 
     c_wd = sel(T.wd[:], T.ones[0:16, :], [[-1, 288]], A.is_equal, 15, 16, f_one)
+    c_id = sel(T.ident[:], T.ones[:, 0:128], [[-1, 128]], A.is_equal, 0, 1)
+    c_m3 = sel(T.m3[:], T.m3[:], [[-1, 16], [-16, 8], [0, 16]], A.is_equal, 0, 1, f_m3)
     t0 = sel(T.bt[:], T.ones[:, 0:128], [[-16, 8], [0, 16]], A.is_ge, 0, 1)
     c_b = sel(T.bm[:], T.bt[:], [[16, 8], [0, 16]], A.is_ge, 15, -1, t0)
     sel(T.lm[:], T.bm[:], [[1, 128]], A.is_gt, 0, -1, c_b)
     c_lu = sel(T.um[:], T.bm[:], [[-1, 128]], A.is_ge, 0, 1)
-    c_id = sel(T.ident[:], T.ones[:, 0:128], [[-1, 128]], A.is_equal, 0, 1)
-    c_m3 = sel(T.m3[:], T.m3[:], [[-1, 16], [-16, 8], [0, 16]], A.is_equal, 0, 1, f_m3)
     done("g", g.iota(T.pi[:], [[0, 1]], 0, 1))
     done("g", g.iota(T.ml[:], [[0, 2], [1, 16]], 0, 0, allow_small_or_imprecise_dtypes=True))
     c_io = done("g", g.iota(T.hi192[:], [[NC, 32]], 0, 0, allow_small_or_imprecise_dtypes=True))
@@ -142,25 +150,38 @@ def rank_program(g, core, T, topo):
             o = 128 * h + 15 - q
             t_k = mm(T.mis[:, 96 * h:96 * h + 96], T.wd[:, o:o + 128], T.sl_h[:, q:1536:16], q == 0, q == 15, v0, c_wd)
 
-    st = {"lane": None, "wm": None}
+    st = {"lane": None, "wm": None, "ab0": None, "ab1": None}
 
-    def one_hot(dig, k, dep):
-        t = None
-        for d in range(8 * k, 8 * k + 8):
-            t = ts(T.oh[:, NC * d:NC * d + NC], dig, float(d), None, A.is_equal, None, dep)
-        need("v", t, f_zero)
-        a = GRP * k
-        init = -128.0 if k == 0 else T.ct[:, a:a + 1]
-        return done("v", V.tensor_tensor_scan(T.ct[:, a + 1:a + GRP + 1], T.oh[:, a:a + GRP], T.zero[:], init, A.add, A.add))
+    def arrivals(r):
+        src = T.cores[r]
+        offs = [d for d in T.cores[r + 1:] if d not in topo.cores_of(src)]
+        eng = topo.engines(src, core)
+        if core not in offs and offs:
+            eng = [e for e in eng if e not in topo.engines(src, offs[0])]
+        return len(eng)
 
-    def sort_pass(dig, off, dep, ps_free, after_counts):
-        sc, ml = [None] * 4, [None] * 4
+    def sort_pass(dig, off, dep, ps_free, first, after_counts, before_last, before_off):
+        sc, ml, oh = [None] * 4, [None] * 4, [None] * 4
         free = list(ps_free)
         acc_t = [None]
         ps = [T.psa, T.psb]
 
+        def one_hot(k):
+            if k in ON_SCALAR:
+                ab = "ab%d" % (k % 2)
+                t = None
+                for i in range(8):
+                    t = act2(T[ab][:, NC * i:NC * i + NC], dig, ACT.Abs, -float(8 * k + i), 1.0, dep, st[ab])
+                oh[k] = st[ab] = act2(T.oh[:, GRP * k:GRP * k + GRP], T[ab][:], ACT.Relu, 1.0, -1.0, t)
+            else:
+                for d in range(8 * k, 8 * k + 8):
+                    oh[k] = ts(T.oh[:, NC * d:NC * d + NC], dig, float(d), None, A.is_equal, None, dep)
+
         def counts(k):
-            sc[k] = one_hot(dig, k, dep if k == 0 else sc[k - 1])
+            a = GRP * k
+            need("v", oh[k], f_zero, sc[k - 1] if k else None)
+            init = -128.0 if k == 0 else T.ct[:, a:a + 1]
+            sc[k] = done("v", V.tensor_tensor_scan(T.ct[:, a + 1:a + GRP + 1], T.oh[:, a:a + GRP], T.zero[:], init, A.add, A.add))
 
         def sums(k):
             t = None
@@ -170,17 +191,28 @@ def rank_program(g, core, T, topo):
                 t = mm(ps[k % 2][:, 512 * b:512 * b + 512], T.um[:], T.ct[:, a:a + 512], False, True)
             return t
 
-        def pick(k, t):
-            a = GRP * k
-            ml[k] = tt(T.msk[:, a:a + GRP], ps[k % 2][:], T.oh[:, a:a + GRP], A.mult, t)
-            free[k % 2] = ml[k]
+        def pick(k, t, parts=1):
+            n = GRP // parts
+            ml[k] = []
+            for i in range(parts):
+                a = GRP * k + n * i
+                ml[k].append(tt(T.msk[:, a:a + n], ps[k % 2][:, n * i:n * i + n], T.oh[:, a:a + n], A.mult, t))
+            free[k % 2] = ml[k][-1]
 
         def reduce_(k):
             for d in range(8 * k, 8 * k + 8):
-                acc_t[0] = mm(T.acc[:, 0:NC], T.ident[:], T.msk[:, NC * d:NC * d + NC], d == 0, d == ND - 1, ml[k], c_id)
+                t = ml[k][(d - 8 * k) * len(ml[k]) // 8]
+                acc_t[0] = mm(T.acc[:, 0:NC], T.ident[:], T.msk[:, NC * d:NC * d + NC], d == 0, d == ND - 1, t, c_id)
 
+        one_hot(0)
+        one_hot(2)
+        t = first()
+        if t is not None:
+            free[1] = t
+        one_hot(3)
         counts(0)
         u0 = sums(0)
+        one_hot(1)
         counts(1)
         u1 = sums(1)
         pick(0, u0)
@@ -191,105 +223,130 @@ def rank_program(g, core, T, topo):
         reduce_(1)
         counts(3)
         u3 = sums(3)
-        if after_counts is not None:
-            after_counts(sc[3])
+        after_counts(sc[3])
         pick(2, u2)
         reduce_(2)
-        pick(3, u3)
+        pick(3, u3, 2)
+        before_last(free)
         reduce_(3)
-        return ts(off[:], T.acc[:, 0:NC], 2048.0, None, A.add, None, acc_t[0]), sc[3], ml[3], free
+        before_off()
+        return ts(off[:], T.acc[:, 0:NC], 2048.0, None, A.add, None, acc_t[0]), free, sc[3]
 
-    def layer(li, src, src_toks, key_tok, out, half_done):
+    def layer(li, src, src_toks, key_tok, out, piece_done):
         v = vcopy(T.ki[:], T.mis[:, 0:NC], key_tok)
         v_lo = ts(T.loi[:], T.ki[:], 31, None, A.bitwise_and, None, v)
-        v_key = ts(T.keyi[:], T.ki[:], 1023, None, A.bitwise_and, None, v)
         v_hi = ts(T.hii[:], T.ki[:], 1023, 5, A.bitwise_and, A.logical_shift_right, v)
+        v_key = ts(T.keyi[:], T.ki[:], 1023, None, A.bitwise_and, None, v)
         v_d1 = vcopy(T.dig1[:], T.loi[:], v_lo)
         v_h16 = ts(T.h16[:], T.hii[:], 16.0, None, A.mult, None, v_hi)
-        v_ko = vcopy(T.koff[:], T.keyi[:], v_key)
-        v_pk = tt(T.pk[:], T.keyi[:], T.h16[:], A.add, v_h16)
-        free = []
-        for h, ps in enumerate((T.psa, T.psb)):
+        v_pk = tt(T.pk[:], T.keyi[:], T.h16[:], A.add, v_key, v_h16)
+
+        def row_bank(ps, b, c, with_src, dep):
             t = None
-            for b in range(3):
-                c = 1536 * h + 512 * b
-                mm(ps[:, 512 * b:512 * b + 512], T.ident[:], src[:, c:c + 512], True, False, c_id, *src_toks)
-                for q in range(16):
-                    t = mm(ps[:, 512 * b + q:512 * b + 512:16], T.m3[:, 128 * q:128 * q + 128],
-                           T.pk[:, c // 16:c // 16 + 32], False, q == 15, v_pk, c_m3)
-            free.append(act(T.packed[:, 1536 * h:1536 * h + 1536], ps[:], t))
-        t_pk = free[1]
+            if with_src:
+                mm(ps[:, 512 * b:512 * b + 512], T.ident[:], src[:, c:c + 512], True, False, c_id, dep, *src_toks)
+            for q in range(16):
+                t = mm(ps[:, 512 * b + q:512 * b + 512:16], T.m3[:, 128 * q:128 * q + 128], T.pk[:, c // 16:c // 16 + 32],
+                       not with_src, q == 15 or not with_src, v_pk, c_m3, dep)
+            return t
 
-        if st["lane"] is None:
-            v = ts(T.li[:], T.pi[:], 15, None, A.bitwise_and, None, c_io)
-            v = vcopy(T.lane[:], T.li[:], v)
-            st["lane"] = ts(T.dq[:], T.ml[:], T.lane[:], None, A.is_equal, None, v)
+        t = None
+        for b in range(3):
+            t = row_bank(T.psb, b, 512 * b, True, None)
+        t_p = [t, None]
 
-        jt = [None]
+        def first():
+            t_p[0] = act(T.packed[:, 0:1536], T.psb[:], t_p[0])
+            return t_p[0]
+
+        jt, cp, ko = [None], [], []
 
         def borders(tok):
             if sends:
                 jt[0] = mm(T.mis[:, 0:32], T.bm[:], T.ct[:, NC:F + 1:NC], True, True, tok)
 
-        v_o1, _, v_m, free = sort_pass(T.dig1[:], T.off1, v_d1, free, borders)
+        def second(free):
+            cp.append(row_bank(T.psa, 0, 1536, True, free[0]))
+
+        def fillers():
+            ko.append(vcopy(T.koff[:], T.keyi[:], v_key))
+            if st["lane"] is None:
+                v = ts(T.li[:], T.pi[:], 15, None, A.bitwise_and, None, c_io)
+                v = vcopy(T.lane[:], T.li[:], v)
+                st["lane"] = ts(T.dq[:], T.ml[:], T.lane[:], None, A.is_equal, None, v)
+                st["wm"] = ts(T.wm[:], T.m2[:], T.wc[:], None, A.mult, None, t_w, c_m2)
+
+        v_o1, free, _ = sort_pass(T.dig1[:], T.off1, v_d1, [None, None], first, borders, second, fillers)
+        for b in (1, 2):
+            cp.append(row_bank(T.psa, b, 1536 + 512 * b, True, None))
+        for b in range(3):
+            t_p[1] = act(T.packed[:, 1536 + 512 * b:2048 + 512 * b], T.psa[:, 512 * b:512 * b + 512], cp[b])
+        free = [t_p[1], free[1]]
+        v = None
+        for h in range(2):
+            need("v", v_o1, t_p[h], v)
+            v = done("v", V.tensor_copy(T.los[:].indirect(T.off1[:, 96 * h:96 * h + 96]), T.packed[:, 1536 * h:1536 * h + 1536]))
+        v_s1 = v
+        t_hi, v_j = None, None
+        if sends:
+            v_j = ts(T.ji[:], T.mis[:, 0:32], 2048.0, None, A.add, None, jt[0], v_s1)
+        need("v", v_s1)
+        for i in range(2):
+            for h in range(2):
+                c = 1536 * h + 768 * i
+                if h == 0:
+                    t = ts(T.ext[:, c:c + 768], T.los[:, c:c + 768], 1.0 / (16.0 * HI), -0.32 / 16.0, A.mult, A.add)
+                else:
+                    t = act2(T.ext[:, c:c + 768], T.los[:, c:c + 768], ACT.Copy, -0.32 / 16.0, 1.0 / (16.0 * HI), v_s1)
+                for q in range(16):
+                    t_hi = mm(T.mis[:, c // 16:c // 16 + 48], T.m2[:, 128 * q:128 * q + 128], T.ext[:, c + q:c + 768:16],
+                              q == 0, q == 15, t, c_m2, v_j)
+        v_l, v_mk = None, None
+        if sends:
+            v_q = ts(T.jq[:], T.ji[:], 15, None, A.bitwise_and, None, v_j)
+            v_c = ts(T.jc[:], T.ji[:], 4, None, A.logical_shift_right, None, v_j)
+            v_mk = ts(T.mk[:], T.jq[:], T.lane[:], None, A.is_gt, None, v_q, st["lane"])
+            v = tt(T.jt[:], T.jc[:], T.dq[:], A.mult, v_c, st["lane"])
+            need("v", v)
+            for b in range(2):
+                v = done("v", V.tensor_reduce(T.cw[:, b:b + 1], T.jt[:, 16 * b:16 * b + 16], AxisListType.X, A.add))
+        v2 = vcopy(T.hii[:], T.mis[:, 0:NC], t_hi)
+        v_d2 = vcopy(T.dig2[:], T.hii[:], v2)
+        if sends:
+            for b in range(2):
+                v_l = ts(T.lst[:, b:64:2], T.hi192[:], T.cw[:, b:b + 1], None, A.add, None, v, c_io)
+
+        def nothing(*a):
+            return None
+
+        v_o2, free, v_ct = sort_pass(T.dig2[:], T.off2, v_d2, free, nothing, nothing, nothing, nothing)
+        t_e = None
+        if sends:
+            s_m = None
+            for d in range(32):
+                q = d % 16
+                s_m = act2(T.ms[:, 128 * d:128 * d + 128], T.m2[:, 128 * q:128 * q + 128], ACT.Identity, 0.0, T.mk[:, d:d + 1],
+                           v_mk, c_m2)
+            need("s", v_l, v_ct)
+            s_1 = done("s", S.activation(T.g1[:], T.ct[:].indirect(T.lst[:]), ACT.Copy))
+            s_2 = done("s", S.activation(T.g2[:], T.oh[:].indirect(T.lst[:]), ACT.Copy))
+            for q in range(16):
+                mm(T.mis[:, 0:64], T.m2[:, 128 * q:128 * q + 128], T.g1[:, q:1024:16], q == 0, False, s_1, v2)
+            for d in range(32):
+                t_e = mm(T.mis[:, d // 16:64:2], T.ms[:, 128 * d:128 * d + 128], T.g2[:, d:1024:32], False, d == 31, s_2, s_m)
+        need("v", v_o2)
+        v = done("v", V.tensor_copy(T.packed[:].indirect(T.off2[:]), T.los[:]))
         t_kr = []
         for h, ps in enumerate((T.psa, T.psb)):
             t = None
             for b in range(3):
-                for q in range(16):
-                    c = 1536 * h + 512 * b
-                    t = mm(ps[:, 512 * b + q:512 * b + 512:16], T.m3[:, 128 * q:128 * q + 128],
-                           T.pk[:, c // 16:c // 16 + 32], True, True, free[h])
+                t = row_bank(ps, b, 1536 * h + 512 * b, False, free[h])
             t_kr.append(act(T.krow[:, 1536 * h:1536 * h + 1536], ps[:], t))
-        need("v", v_o1, t_pk)
-        v_s1 = done("v", V.tensor_copy(T.los[:].indirect(T.off1[:]), T.packed[:]))
-        t_hi, v_j = None, None
-        if sends:
-            v_j = ts(T.ji[:], T.mis[:, 0:32], 2048.0, None, A.add, None, jt[0])
-        for h in range(2):
-            need("s", v_s1)
-            t = done("s", S.activation(T.ext[:, 1536 * h:1536 * h + 1536], T.los[:, 1536 * h:1536 * h + 1536], ACT.Copy,
-                                       bias=-0.32 / 16.0, scale=1.0 / (16.0 * HI)))
-            for q in range(16):
-                t_hi = mm(T.mis[:, 96 * h:96 * h + 96], T.m2[:, 128 * q:128 * q + 128],
-                          T.ext[:, 1536 * h + q:1536 * h + 1536:16], q == 0, q == 15, t, c_m2, v_j)
-        if sends:
-            v_q = ts(T.jq[:], T.ji[:], 15, None, A.bitwise_and, None, v_j)
-            v_c = ts(T.jc[:], T.ji[:], 4, None, A.logical_shift_right, None, v_j)
-            v = tt(T.jt[:], T.jc[:], T.dq[:], A.mult, v_c, st["lane"])
-            v_mk = ts(T.mk[:, 0:32], T.jq[:], T.lane[:], None, A.is_gt, None, v_q)
-            need("v", v)
-            for b in range(2):
-                v = done("v", V.tensor_reduce(T.cw[:, b:b + 1], T.jt[:, 16 * b:16 * b + 16], AxisListType.X, A.add))
-            for b in range(2):
-                v_l = ts(T.lst[:, b:64:2], T.hi192[:], T.cw[:, b:b + 1], None, A.add, None, v, c_io)
-            s_mk, n = v_mk, 32
-            while n < 1024:
-                s_mk = act(T.mk[:, n:2 * n], T.mk[:, 0:n], s_mk)
-                n *= 2
-        if st["wm"] is None:
-            st["wm"] = ts(T.wm[:], T.m2[:], T.wc[:], None, A.mult, None, t_w, c_m2)
-        v = vcopy(T.hii[:], T.mis[:, 0:NC], t_hi)
-        v_d2 = vcopy(T.dig2[:], T.hii[:], v)
-
-        v_o2, v_sc, v_m, free = sort_pass(T.dig2[:], T.off2, v_d2, t_kr, None)
-        t_e = None
-        if sends:
-            need("s", v_sc, v_l)
-            s_g = done("s", S.activation(T.g1[:], T.ct[:].indirect(T.lst[:]), ACT.Copy))
-            v_g = tt(T.g2[:], T.oh[:].indirect(T.lst[:]), T.mk[:], A.mult, s_mk, v_l)
-            for q in range(16):
-                mm(T.mis[:, 0:64], T.m2[:, 128 * q:128 * q + 128], T.g1[:, q:1024:16], q == 0, False, s_g)
-            for q in range(16):
-                t_e = mm(T.mis[:, 0:64], T.m2[:, 128 * q:128 * q + 128], T.g2[:, q:1024:16], False, q == 15, v_g)
-        need("v", v_o2)
-        v = done("v", V.tensor_copy(T.packed[:].indirect(T.off2[:]), T.los[:]))
-        if sends:
-            v_e = ts(T.eoff[:], T.mis[:, 0:64], 2055.0, None, A.add, None, t_e)
         need("v", v)
         v_mx = done("v", V.tensor_tensor_scan(T.srt[:, 8:], T.packed[:], T.packed[:], NEG, A.max, A.max))
         tl = T["tl%d" % li]
         if sends:
+            v_e = ts(T.eoff[:], T.mis[:, 0:64], 2055.0, None, A.add, None, t_e)
             v_t = tt(tl[:], T.srt[:].indirect(T.eoff[:]), T.kc[:], A.subtract, v_mx, v_e, c_kc)
             need("g", v_t)
             off_chip, on_chip = [], []
@@ -315,63 +372,52 @@ def rank_program(g, core, T, topo):
         v_a = done("v", V.tensor_copy(T.los[:, 0:16 * a], T.srt[:, 8:].indirect(T.off2[:, 0:a])))
         need("s", v_mx)
         s_a = done("s", S.activation(T.los[:, 16 * a:], T.srt[:, 8:].indirect(T.off2[:, a:NC]), ACT.Copy))
-        tin, v_in = None, None
+        dst = T.yl if rank > 0 else out
+        ys = []
+        for c, e in ((CUT, S_TOK), (0, CUT)):
+            need("v", v_a, s_a, t_kr[1])
+            ys.append(done("v", V.tensor_tensor(dst[:, c:e], T.los[:].indirect(T.off1[:, c // 16:e // 16]), T.krow[:, c:e], A.subtract)))
+            if rank == 0:
+                piece_done(c, e, ys[-1])
         if rank > 0:
-            def landed(r):
-                d = T.cores[r]
-                n = 8
-                return ("r%d%d" % (li, r), arrivals(r))
-
-            def arrivals(r):
-                src_core = T.cores[r]
-                ups = T.cores[r + 1:]
-                offs = [d for d in ups if d not in topo.cores_of(src_core)]
-                if core in offs:
-                    return len(topo.engines(src_core, core))
-                taken = topo.engines(src_core, offs[0]) if offs else []
-                return len([e for e in topo.engines(src_core, core) if e not in taken])
+            parts, c = [], CUT
+            for ps, o in ((T.acc, 0), (T.psa, 1024), (T.psb, 1024)):
+                n = min(512, S_TOK - c)
+                t = mm(ps[:, o:o + n], T.ident[:], T.yl[:, c:c + n], True, True, ys[0], t_kr[1])
+                parts.append((ps, o, c, n, t))
+                c += n
             tin = T["ld%d0" % li]
-            v_in = landed(0)
+            v_in = ("r%d0" % li, arrivals(0))
+            merge = []
             for r in range(1, rank):
                 ps = (T.psa, T.psb)[r % 2]
                 for b in range(2):
                     t = mm(ps[:, 512 * b:512 * b + 512], T.ident[:], T["ld%d%d" % (li, r)][:, 512 * b:512 * b + 512], True, True,
-                           landed(r), v_m)
-                nxt = (T.ta, T.tb)[r % 2]
-                st["mx%d" % r] = (nxt, ps, t)
-        dst = T.yl if rank > 0 else out
-        ys = []
-        for h in range(2):
-            need("v", v_a, s_a, t_kr[1])
-            c = 1536 * h
-            ys.append(done("v", V.tensor_tensor(dst[:, c:c + 1536], T.los[:].indirect(T.off1[:, 96 * h:96 * h + 96]),
-                                                T.krow[:, c:c + 1536], A.subtract)))
-            if rank == 0:
-                half_done(h, ys[h])
-        if rank > 0:
-            for r in range(1, rank):
-                nxt, ps, t = st["mx%d" % r]
+                           ("r%d%d" % (li, r), arrivals(r)), t_kr[r % 2])
+                merge.append(((T.ta, T.tb)[r % 2], ps, t))
+            for nxt, ps, t in merge:
                 v_in = tt(nxt[:], ps[:, 0:1024], tin[:], A.max, t, v_in)
                 tin = nxt
-            for h in range(2):
-                c = 1536 * h
-                half_done(h, tt(out[:, c:c + 1536], tin[:].indirect(T.koff[:, 96 * h:96 * h + 96]), T.yl[:, c:c + 1536], A.max,
-                                v_in, ys[h], v_ko))
+            need("s", v_in, ko[0])
+            s_t = done("s", S.activation(T.ext[:, CUT:], tin[:].indirect(T.koff[:, CUT // 16:]), ACT.Copy))
+            piece_done(0, CUT, tt(out[:, 0:CUT], tin[:].indirect(T.koff[:, 0:CUT // 16]), T.yl[:, 0:CUT], A.max, v_in, ys[1], ko[0]))
+            for ps, o, c, n, t in parts:
+                v = tt(out[:, c:c + n], ps[:, o:o + n], T.ext[:, c:c + n], A.max, t, s_t)
+            piece_done(CUT, S_TOK, v)
 
-    hk = {}
+    hk = []
 
-    def hash_half(h, tok):
-        hk[h] = tok
+    def hash_piece(c, e, tok):
+        t = None
         for q in range(16):
-            hk["t"] = mm(T.mis[:, 96 * h:96 * h + 96], T.wm[:, 128 * q:128 * q + 128], T.y1[:, 1536 * h + q:1536 * h + 1536:16],
-                         q == 0, q == 15, tok, st["wm"])
+            t = mm(T.mis[:, c // 16:e // 16], T.wm[:, 128 * q:128 * q + 128], T.y1[:, c + q:e:16], q == 0, q == 15, tok, st["wm"])
+        hk.append((tok, t))
 
-    def store_half(h, tok):
-        c = 1536 * h
-        dma("y", "dy%d" % h, T.y[:, c:c + 1536], T.yo[:, c:c + 1536], tok)
+    def store_piece(c, e, tok):
+        dma("y", "dy0" if c else "dy1", T.y[:, c:e], T.yo[:, c:e], tok)
 
-    layer(0, T.xs, t_x, t_k, T.y1, hash_half)
-    layer(1, T.y1, [hk[0], hk[1]], hk["t"], T.yo, store_half)
+    layer(0, T.xs, t_x, t_k, T.y1, hash_piece)
+    layer(1, T.y1, [hk[0][0], hk[1][0]], hk[1][1], T.yo, store_piece)
 
     for q in ("v", "s", "p", "g"):
         need("g", ("c" + q, count[q]))

@@ -3,11 +3,18 @@ from concourse.mybir import dt, AluOpType, AxisListType, ActivationFunctionType
 
 S_TOK, NC, ND = 3072, 192, 32
 F = NC * ND
-GRP = 8 * NC
 HI = 24576
 NEG = -1000000.0
-ON_SCALAR = (2, 3)
-CUT = 1792
+MAGIC = 12582912.0
+ND_V = 20
+MID = (ND_V + ND) // 2
+F_V = NC * ND_V
+FS = F - F_V
+EV = 96
+SHIFT = 1024.0
+SC_V = 104
+STORE = 2688
+CUT = 1664
 
 SCRATCH = {
     "sl_i": ("sbuf", [16, 1536], "int32"), "sl_h": ("sbuf", [16, 1536], "float16"),
@@ -17,32 +24,38 @@ SCRATCH = {
     "ones": ("sbuf", [128, 288], "bfloat16"), "wd": ("sbuf", [16, 288], "bfloat16"),
     "ident": ("sbuf", [128, 128], "bfloat16"), "bm": ("sbuf", [128, 128], "bfloat16"), "bt": ("sbuf", [128, 128], "bfloat16"),
     "lm": ("sbuf", [128, 128], "bfloat16"), "um": ("sbuf", [128, 128], "bfloat16"),
+    "i192": ("sbuf", [128, 128], "bfloat16"), "cio": ("sbuf", [128, NC], "bfloat16"),
     "m2": ("sbuf", [128, 2048], "bfloat16"), "m3": ("sbuf", [128, 2048], "bfloat16"), "wm": ("sbuf", [128, 2048], "bfloat16"),
-    "ms": ("sbuf", [128, 4096], "bfloat16"),
+    "m2l": ("sbuf", [128, 2048], "bfloat16"),
+    "dl": ("sbuf", [128, NC], "bfloat16"), "sq": ("sbuf", [128, NC], "bfloat16"),
+    "dgm": ("sbuf", [128, 128 * (ND - ND_V)], "bfloat16"), "e2r": ("sbuf", [1, 1536], "bfloat16"),
     "pi": ("sbuf", [128, 1], "int32"), "li": ("sbuf", [128, 1], "int32"), "lane": ("sbuf", [128, 1], "float32"),
     "ml": ("sbuf", [128, 32], "float32"), "dq": ("sbuf", [128, 32], "float32"), "hi192": ("sbuf", [128, 32], "float32"),
-    "kc": ("sbuf", [128, 1024], "float32"), "zero": ("sbuf", [128, GRP], "bfloat16"),
-    "ki": ("sbuf", [128, NC], "int32"), "loi": ("sbuf", [128, NC], "int32"), "hii": ("sbuf", [128, NC], "int32"),
-    "keyi": ("sbuf", [128, NC], "int32"), "h16": ("sbuf", [128, NC], "float32"), "pk": ("sbuf", [128, NC], "float16"),
+    "kc": ("sbuf", [128, 1024], "float32"), "zero": ("sbuf", [128, 3072], "bfloat16"),
+    "ki": ("sbuf", [128, NC], "int32"), "loi": ("sbuf", [128, NC], "int32"),
+    "keyi": ("sbuf", [128, NC], "int32"), "h16": ("sbuf", [128, NC], "int32"), "pk": ("sbuf", [128, NC], "float16"),
     "dig1": ("sbuf", [128, NC], "bfloat16"), "dig2": ("sbuf", [128, NC], "bfloat16"), "koff": ("sbuf", [128, NC], "uint16"),
+    "poff": ("sbuf", [128, EV], "uint16"),
     "off1": ("sbuf", [128, NC], "uint16"), "off2": ("sbuf", [128, NC], "uint16"),
     "eoff": ("sbuf", [128, 64], "uint16"), "lst": ("sbuf", [128, 64], "uint16"),
-    "oh": ("sbuf", [128, F + 16], "bfloat16"), "ct": ("sbuf", [128, F + 16], "bfloat16"), "msk": ("sbuf", [128, F], "float16"),
-    "ab0": ("sbuf", [128, GRP], "bfloat16"), "ab1": ("sbuf", [128, GRP], "bfloat16"),
+    "oh": ("sbuf", [128, F + 16], "bfloat16"), "ct": ("sbuf", [128, F + 16], "bfloat16"),
+    "msk": ("sbuf", [128, ND * EV], "float16"),
+    "g1": ("sbuf", [128, 16 * EV], "bfloat16"), "g2": ("sbuf", [128, 16 * EV], "bfloat16"),
     "ji": ("sbuf", [128, 32], "int32"), "jq": ("sbuf", [128, 32], "int32"), "jc": ("sbuf", [128, 32], "int32"),
-    "jt": ("sbuf", [128, 32], "float32"), "cw": ("sbuf", [128, 2], "float32"), "mk": ("sbuf", [128, 32], "float32"),
-    "g1": ("sbuf", [128, 1024], "bfloat16"), "g2": ("sbuf", [128, 1024], "bfloat16"),
-    "packed": ("sbuf", [128, S_TOK], "float32"), "krow": ("sbuf", [128, S_TOK], "float32"),
+    "jt": ("sbuf", [128, 32], "float32"), "cw": ("sbuf", [128, 2], "float32"), "mkt": ("sbuf", [128, 1024], "bfloat16"),
+    "e1": ("sbuf", [128, 1024], "bfloat16"), "e2": ("sbuf", [128, 1024], "bfloat16"), "e3": ("sbuf", [128, 1024], "bfloat16"),
+    "packed": ("sbuf", [128, S_TOK], "float32"), "pkb": ("sbuf", [128, S_TOK], "float32"),
+    "krow": ("sbuf", [128, S_TOK], "float32"),
     "los": ("sbuf", [128, S_TOK], "float32"), "ext": ("sbuf", [128, S_TOK], "bfloat16"),
     "srt": ("sbuf", [128, S_TOK + 8], "float32"),
     "tl0": ("sbuf", [128, 1024], "bfloat16"), "tl1": ("sbuf", [128, 1024], "bfloat16"),
     "ld00": ("sbuf", [128, 1024], "bfloat16"), "ld01": ("sbuf", [128, 1024], "bfloat16"), "ld02": ("sbuf", [128, 1024], "bfloat16"),
     "ld10": ("sbuf", [128, 1024], "bfloat16"), "ld11": ("sbuf", [128, 1024], "bfloat16"), "ld12": ("sbuf", [128, 1024], "bfloat16"),
     "ta": ("sbuf", [128, 1024], "bfloat16"), "tb": ("sbuf", [128, 1024], "bfloat16"),
-    "psa": ("psum", [128, GRP], "float32"), "psb": ("psum", [128, GRP], "float32"),
+    "psa": ("psum", [128, 1536], "float32"), "psb": ("psum", [128, 1536], "float32"),
     "acc": ("psum", [128, 512], "float32"), "mis": ("psum", [128, 512], "float32"),
 }
-SEMAPHORES = (["cv", "cs", "cp", "cg", "dx0", "dx1", "ds0", "ds1", "dw", "dy0", "dy1", "lo0", "lo1"]
+SEMAPHORES = (["cv", "cs", "cp", "cg", "dx0", "dx1", "ds0", "ds1", "dw", "dy0", "dy1", "dy2", "lo0", "lo1"]
               + ["r%d%d" % (a, b) for a in range(2) for b in range(3)])
 
 
@@ -117,12 +130,8 @@ def rank_program(g, core, T, topo):
 
     f_one = fill(T.ones[:], 1.0)
     f_m3 = fill(T.m3[:], 512.0)
-    fill(T.ct[:, 0:1], -128.0)
-    fill(T.ct[:, F + 1:F + 16], 0.0)
-    fill(T.oh[:, F:F + 16], 0.0)
-    fill(T.srt[:, 0:8], NEG)
-    f_zero = fill(T.zero[:], 0.0)
-    f_m2 = fill(T.m2[:], 1.0)
+    f_m2 = fill(T.m2[:], 0.0)
+    f_m2l = fill(T.m2l[:], 0.0)
 
     def sel(out, in_, pattern, op, base, cm, *deps):
         need("g", *deps)
@@ -130,164 +139,188 @@ def rank_program(g, core, T, topo):
 
     c_wd = sel(T.wd[:], T.ones[0:16, :], [[-1, 288]], A.is_equal, 15, 16, f_one)
     c_id = sel(T.ident[:], T.ones[:, 0:128], [[-1, 128]], A.is_equal, 0, 1)
-    c_m3 = sel(T.m3[:], T.m3[:], [[-1, 16], [-16, 8], [0, 16]], A.is_equal, 0, 1, f_m3)
     t0 = sel(T.bt[:], T.ones[:, 0:128], [[-16, 8], [0, 16]], A.is_ge, 0, 1)
     c_b = sel(T.bm[:], T.bt[:], [[16, 8], [0, 16]], A.is_ge, 15, -1, t0)
-    sel(T.lm[:], T.bm[:], [[1, 128]], A.is_gt, 0, -1, c_b)
-    c_lu = sel(T.um[:], T.bm[:], [[-1, 128]], A.is_ge, 0, 1)
+    c_lm = sel(T.lm[:], T.bm[:], [[1, 128]], A.is_gt, 0, -1, c_b)
+    c_um = sel(T.um[:], T.bm[:], [[-1, 128]], A.is_ge, 0, 1)
+    c_m3 = sel(T.m3[:], T.m3[:], [[-1, 16], [-16, 8], [0, 16]], A.is_equal, 0, 1, f_m3)
+    c_cio = done("g", g.iota(T.cio[:], [[1, NC]], 0, 0, allow_small_or_imprecise_dtypes=True))
     done("g", g.iota(T.pi[:], [[0, 1]], 0, 1))
     done("g", g.iota(T.ml[:], [[0, 2], [1, 16]], 0, 0, allow_small_or_imprecise_dtypes=True))
     c_io = done("g", g.iota(T.hi192[:], [[NC, 32]], 0, 0, allow_small_or_imprecise_dtypes=True))
-    t0 = sel(T.m2[:], T.m2[:], [[-1, 16], [0, 8], [1, 16]], A.is_equal, 0, 0, f_m2)
-    t0 = sel(T.m2[:], T.m2[:], [[0, 16], [-16, 8], [0, 16]], A.is_ge, 0, 1, t0)
-    c_m2 = sel(T.m2[:], T.m2[:], [[0, 16], [16, 8], [0, 16]], A.is_ge, 15, -1, t0)
-    c_kc = done("g", g.iota(T.kc[:], [[HI, 32], [512, 32]], 0, 0, allow_small_or_imprecise_dtypes=True))
+    c_kc = done("g", g.iota(T.kc[:], [[HI, 32], [512, 32]], int(SHIFT), 0, allow_small_or_imprecise_dtypes=True))
+    c_m2 = None
+    for q in range(16):
+        act(T.m2[:, 128 * q + q:128 * q + 128:16], T.bm[:, q:128:16], c_b, f_m2)
+    for q in range(16):
+        c_m2 = act(T.m2l[:, 128 * q + q:128 * q + 128:16], T.lm[:, q:128:16], c_lm, f_m2l)
+    c_192 = act2(T.i192[:], T.ident[:], ACT.Silu, 0.0, 192.0, c_id)
+    c_dg = None
+    for i in range(ND - ND_V):
+        c_dg = act2(T.dgm[:, 128 * i:128 * i + 128], T.ident[:], ACT.Copy, 0.0, -2.0 * (ND_V + i - MID), c_id)
 
     t_k = None
-    v0 = vcopy(T.sl_h[:], T.sl_i[:], *t_s)
-    for h in range(2):
-        for q in range(16):
-            o = 128 * h + 15 - q
-            t_k = mm(T.mis[:, 96 * h:96 * h + 96], T.wd[:, o:o + 128], T.sl_h[:, q:1536:16], q == 0, q == 15, v0, c_wd)
+    for i in range(2):
+        v0 = vcopy(T.sl_h[:, 768 * i:768 * i + 768], T.sl_i[:, 768 * i:768 * i + 768], *t_s)
+        for h in range(2):
+            for q in range(16):
+                o, c = 128 * h + 15 - q, 96 * h + 48 * i
+                t_k = mm(T.mis[:, c:c + 48], T.wd[:, o:o + 128], T.sl_h[:, 768 * i + q:768 * i + 768:16], q == 0, q == 15, v0, c_wd)
+    fill(T.ct[:, 0:1], -128.0)
+    fill(T.zero[:], 0.0)
+    fill(T.ct[:, F + 1:F + 16], 0.0)
+    fill(T.oh[:, F:F + 16], 0.0)
+    f_end = fill(T.srt[:, 0:8], NEG)
+    for e in range(1, MID - ND_V + 1):
+        f_end = fill(T.e2r[:, 128 * e:128 * e + 128], float(e * e))
 
-    st = {"lane": None, "wm": None, "ab0": None, "ab1": None}
+    def low(buf, *deps):
+        need("g", *deps)
+        return done("g", g.iota(buf[:], [[0, S_TOK]], int(NEG), 0, allow_small_or_imprecise_dtypes=True))
+
+    st = {"lane": None, "wm": None, "mx": None}
+
+    def off_chip_of(src):
+        r = T.rank_of(src)
+        return [d for d in T.cores[r + 1:] if d not in topo.cores_of(src)]
+
+    def link(src, dst):
+        eng = topo.engines(src, dst)
+        offs = off_chip_of(src)
+        if dst in offs:
+            return eng
+        if offs:
+            eng = [e for e in eng if e not in topo.engines(src, offs[0])]
+        return eng[:len(eng) // 2]
 
     def arrivals(r):
-        src = T.cores[r]
-        offs = [d for d in T.cores[r + 1:] if d not in topo.cores_of(src)]
-        eng = topo.engines(src, core)
-        if core not in offs and offs:
-            eng = [e for e in eng if e not in topo.engines(src, offs[0])]
-        return len(eng)
+        return len(link(T.cores[r], core))
 
-    def sort_pass(dig, off, dep, ps_free, first, after_counts, before_last, before_off):
-        sc, ml, oh = [None] * 4, [None] * 4, [None] * 4
-        free = list(ps_free)
-        acc_t = [None]
-        ps = [T.psa, T.psb]
-
-        def one_hot(k):
-            if k in ON_SCALAR:
-                ab = "ab%d" % (k % 2)
-                t = None
-                for i in range(8):
-                    t = act2(T[ab][:, NC * i:NC * i + NC], dig, ACT.Abs, -float(8 * k + i), 1.0, dep, st[ab])
-                oh[k] = st[ab] = act2(T.oh[:, GRP * k:GRP * k + GRP], T[ab][:], ACT.Relu, 1.0, -1.0, t)
-            else:
-                for d in range(8 * k, 8 * k + 8):
-                    oh[k] = ts(T.oh[:, NC * d:NC * d + NC], dig, float(d), None, A.is_equal, None, dep)
-
-        def counts(k):
-            a = GRP * k
-            need("v", oh[k], f_zero, sc[k - 1] if k else None)
-            init = -128.0 if k == 0 else T.ct[:, a:a + 1]
-            sc[k] = done("v", V.tensor_tensor_scan(T.ct[:, a + 1:a + GRP + 1], T.oh[:, a:a + GRP], T.zero[:], init, A.add, A.add))
-
-        def sums(k):
-            t = None
-            for b in range(3):
-                a = GRP * k + 512 * b
-                mm(ps[k % 2][:, 512 * b:512 * b + 512], T.lm[:], T.ct[:, a + 1:a + 513], True, False, sc[k], free[k % 2], c_lu)
-                t = mm(ps[k % 2][:, 512 * b:512 * b + 512], T.um[:], T.ct[:, a:a + 512], False, True)
-            return t
-
-        def pick(k, t, parts=1):
-            n = GRP // parts
-            ml[k] = []
-            for i in range(parts):
-                a = GRP * k + n * i
-                ml[k].append(tt(T.msk[:, a:a + n], ps[k % 2][:, n * i:n * i + n], T.oh[:, a:a + n], A.mult, t))
-            free[k % 2] = ml[k][-1]
-
-        def reduce_(k):
-            for d in range(8 * k, 8 * k + 8):
-                t = ml[k][(d - 8 * k) * len(ml[k]) // 8]
-                acc_t[0] = mm(T.acc[:, 0:NC], T.ident[:], T.msk[:, NC * d:NC * d + NC], d == 0, d == ND - 1, t, c_id)
-
-        one_hot(0)
-        one_hot(2)
-        t = first()
-        if t is not None:
-            free[1] = t
-        one_hot(3)
-        counts(0)
-        u0 = sums(0)
-        one_hot(1)
-        counts(1)
-        u1 = sums(1)
-        pick(0, u0)
-        reduce_(0)
-        counts(2)
-        u2 = sums(2)
-        pick(1, u1)
-        reduce_(1)
-        counts(3)
-        u3 = sums(3)
-        after_counts(sc[3])
-        pick(2, u2)
-        reduce_(2)
-        pick(3, u3, 2)
-        before_last(free)
-        reduce_(3)
-        before_off()
-        return ts(off[:], T.acc[:, 0:NC], 2048.0, None, A.add, None, acc_t[0]), free, sc[3]
+    def sort_pass(dig, off, dep, ps_free, early_v, mid, fillers, late):
+        mm(T.acc[:, 256:256 + EV], T.i192[:], dig[:, 1:NC:2], True, False, dep, c_192)
+        t_po = mm(T.acc[:, 256:256 + EV], T.ident[:], T.cio[:, 1:NC:2], False, True, c_id, c_cio)
+        t_dl = act2(T.dl[:], dig, ACT.Copy, -float(MID), 1.0, dep)
+        t_sq = act2(T.sq[:], dig, ACT.Square, -float(MID), 1.0, dep)
+        n = FS // 512 + (FS % 512 > 0)
+        relu, s_oh = list(ps_free), None
+        for b in range(n):
+            o, w, c, t = 512 * (b % 3), min(512, FS - 512 * b), 512 * b, None
+            while c < 512 * b + w:
+                i = c // NC
+                m = min(NC * (i + 1), 512 * b + w)
+                e = ND_V + i - MID
+                z, k = T.psa[:, o + c - 512 * b:o + m - 512 * b], c - NC * i
+                if e:
+                    mm(z, T.dgm[:, 128 * i:128 * i + 128], T.dl[:, k:k + m - c], True, False, t_dl, c_dg, relu[b % 3])
+                    mm(z, T.e2r[:, 128 * abs(e):128 * abs(e) + 128], T.ones[0:1, 0:m - c], False, False, f_end)
+                t = mm(z, T.ident[:], T.sq[:, k:k + m - c], e == 0, True, t_sq, c_id, relu[b % 3])
+                c = m
+            s_oh = act2(T.oh[:, F_V + 512 * b:F_V + 512 * b + w], T.psa[:, o:o + w], ACT.Relu, 1.0, -1.0, t, f_end)
+            relu[b % 3] = s_oh
+        v_oh, v_po = None, None
+        for d in range(ND_V):
+            if d == 4:
+                early_v()
+            if d == 12:
+                v_po = vcopy(T.poff[:], T.acc[:, 256:256 + EV], t_po)
+            v_oh = ts(T.oh[:, NC * d:NC * d + NC], dig, float(d), None, A.is_equal, None, dep)
+        mid()
+        sc, c, tok = None, 0, {}
+        while c < F:
+            w = min(3072, (F_V if c < F_V else F) - c)
+            need("v", v_oh, sc, s_oh if c >= F_V else None)
+            init = -128.0 if c == 0 else T.ct[:, c:c + 1]
+            sc = done("v", V.tensor_tensor_scan(T.ct[:, c + 1:c + w + 1], T.oh[:, c:c + w], T.zero[:, 0:w], init, A.add, A.add))
+            c += w
+            tok[c] = sc
+        need("s", v_oh, s_oh, v_po)
+        s_2 = done("s", S.activation(T.g2[:], T.oh[:].indirect(T.poff[:]), ACT.Copy))
+        need("s", sc)
+        s_1 = done("s", S.activation(T.g1[:], T.ct[:].indirect(T.poff[:]), ACT.Copy))
+        bank, red, d, t = list(relu), [], 0, None
+        for b in range(6):
+            z, a = T.psa[:, 512 * (b % 3):512 * (b % 3) + 512], 1024 * b
+            t = tok[min(k for k in tok if k >= min(a + 1025, F))]
+            mm(z, T.lm[:], T.ct[:, a + 1:a + 1025:2], True, False, t, c_lm, bank[b % 3])
+            t = mm(z, T.um[:], T.ct[:, a:a + 1024:2], False, True, c_um)
+            bank[b % 3] = tt(T.msk[:, 512 * b:512 * b + 512], z, T.oh[:, a:a + 1024:2], A.mult, t)
+            red.append(bank[b % 3])
+            if b == 3:
+                fillers(sc)
+                for q in range(16):
+                    mm(T.mis[:, 256:256 + EV], T.m2l[:, 128 * q:128 * q + 128], T.g2[:, q:16 * EV:16], q == 0, False, s_2, c_m2)
+            if b in (2, 4, 5):
+                while EV * (d + 1) <= 512 * (b - 1):
+                    mm(T.acc[:, 0:EV], T.ident[:], T.msk[:, EV * d:EV * d + EV], d == 0, False, red[b - 2])
+                    d += 1
+        t_o = None
+        for q in range(16):
+            t_o = mm(T.mis[:, 256:256 + EV], T.m2[:, 128 * q:128 * q + 128], T.g1[:, q:16 * EV:16], False, q == 15, s_1)
+        while d < ND:
+            t = mm(T.acc[:, 0:EV], T.ident[:], T.msk[:, EV * d:EV * d + EV], False, d == ND - 1, red[min(5, (EV * d + EV - 1) // 512)])
+            d += 1
+        late()
+        ts(off[:, 1:NC:2], T.mis[:, 256:256 + EV], 2048.0, None, A.add, None, t_o)
+        return ts(off[:, 0:NC:2], T.acc[:, 0:EV], 2048.0, None, A.add, None, t), sc, bank
 
     def layer(li, src, src_toks, key_tok, out, piece_done):
         v = vcopy(T.ki[:], T.mis[:, 0:NC], key_tok)
         v_lo = ts(T.loi[:], T.ki[:], 31, None, A.bitwise_and, None, v)
-        v_hi = ts(T.hii[:], T.ki[:], 1023, 5, A.bitwise_and, A.logical_shift_right, v)
-        v_key = ts(T.keyi[:], T.ki[:], 1023, None, A.bitwise_and, None, v)
         v_d1 = vcopy(T.dig1[:], T.loi[:], v_lo)
-        v_h16 = ts(T.h16[:], T.hii[:], 16.0, None, A.mult, None, v_hi)
-        v_pk = tt(T.pk[:], T.keyi[:], T.h16[:], A.add, v_key, v_h16)
+        kt, t_p, t_kr, jt, pb, ko = {}, [], [], [None], [], []
 
-        def row_bank(ps, b, c, with_src, dep):
+        def pack_keys():
+            a = ts(T.keyi[:], T.ki[:], 1023, None, A.bitwise_and, None, v)
+            b = ts(T.h16[:], T.ki[:], 992, 1, A.bitwise_and, A.logical_shift_right, v)
+            kt["pk"] = tt(T.pk[:], T.keyi[:], T.h16[:], A.add, a, b)
+            kt["key"] = a
+
+        def row_bank(ps, b, c, with_src, *deps):
             t = None
             if with_src:
-                mm(ps[:, 512 * b:512 * b + 512], T.ident[:], src[:, c:c + 512], True, False, c_id, dep, *src_toks)
+                mm(ps[:, 512 * b:512 * b + 512], T.ident[:], src[:, c:c + 512], True, False, c_id, *(deps + tuple(src_toks)))
             for q in range(16):
                 t = mm(ps[:, 512 * b + q:512 * b + 512:16], T.m3[:, 128 * q:128 * q + 128], T.pk[:, c // 16:c // 16 + 32],
-                       not with_src, q == 15 or not with_src, v_pk, c_m3, dep)
+                       not with_src, q == 15 or not with_src, kt["pk"], c_m3, *deps)
             return t
 
-        t = None
-        for b in range(3):
-            t = row_bank(T.psb, b, 512 * b, True, None)
-        t_p = [t, None]
+        def packs(h, free):
+            for b in range(3):
+                pb.append(row_bank(T.psb, b, 1536 * h + 512 * b, True, free[b]))
+            for b in range(3):
+                t_p.append(act2(T.packed[:, 1536 * h + 512 * b:1536 * h + 512 * b + 512], T.psb[:, 512 * b:512 * b + 512], ACT.Copy,
+                                SHIFT, 1.0, pb[3 * h + b], st["mx"]))
 
-        def first():
-            t_p[0] = act(T.packed[:, 0:1536], T.psb[:], t_p[0])
-            return t_p[0]
-
-        jt, cp, ko = [None], [], []
-
-        def borders(tok):
+        def fillers(sc):
             if sends:
-                jt[0] = mm(T.mis[:, 0:32], T.bm[:], T.ct[:, NC:F + 1:NC], True, True, tok)
-
-        def second(free):
-            cp.append(row_bank(T.psa, 0, 1536, True, free[0]))
-
-        def fillers():
-            ko.append(vcopy(T.koff[:], T.keyi[:], v_key))
+                jt[0] = mm(T.mis[:, 0:32], T.bm[:], T.ct[:, NC:F + 1:NC], True, True, sc)
+            ko.append(vcopy(T.koff[:], T.keyi[:], kt["key"]))
             if st["lane"] is None:
-                v = ts(T.li[:], T.pi[:], 15, None, A.bitwise_and, None, c_io)
-                v = vcopy(T.lane[:], T.li[:], v)
-                st["lane"] = ts(T.dq[:], T.ml[:], T.lane[:], None, A.is_equal, None, v)
-                st["wm"] = ts(T.wm[:], T.m2[:], T.wc[:], None, A.mult, None, t_w, c_m2)
+                a = ts(T.li[:], T.pi[:], 15, None, A.bitwise_and, None, c_io)
+                a = vcopy(T.lane[:], T.li[:], a)
+                st["lane"] = ts(T.dq[:], T.ml[:], T.lane[:], None, A.is_equal, None, a)
 
-        v_o1, free, _ = sort_pass(T.dig1[:], T.off1, v_d1, [None, None], first, borders, second, fillers)
-        for b in (1, 2):
-            cp.append(row_bank(T.psa, b, 1536 + 512 * b, True, None))
-        for b in range(3):
-            t_p[1] = act(T.packed[:, 1536 + 512 * b:2048 + 512 * b], T.psa[:, 512 * b:512 * b + 512], cp[b])
-        free = [t_p[1], free[1]]
+        def nothing(*a):
+            return None
+
+        v_o1, _, psa_t = sort_pass(T.dig1[:], T.off1, v_d1, [None] * 3, pack_keys, lambda: packs(0, [None] * 3), fillers,
+                                   lambda: packs(1, t_p))
         v = None
         for h in range(2):
-            need("v", v_o1, t_p[h], v)
+            need("v", v_o1, t_p[3 * h + 2], v)
             v = done("v", V.tensor_copy(T.los[:].indirect(T.off1[:, 96 * h:96 * h + 96]), T.packed[:, 1536 * h:1536 * h + 1536]))
         v_s1 = v
+        g_b = low(T.pkb, st["mx"])
+        g_a = low(T.packed, v_s1)
+        for h, ps in enumerate((T.psa, T.psb)):
+            t = None
+            for b in range(3):
+                t = row_bank(ps, b, 1536 * h + 512 * b, False, psa_t[b] if h == 0 else t_p[3 + b])
+            t_kr.append(act2(T.krow[:, 1536 * h:1536 * h + 1536], ps[:], ACT.Copy, SHIFT, 1.0, t))
+        if st["wm"] is None:
+            st["wm"] = act2(T.wm[:], T.m2[:], ACT.Copy, 0.0, T.wc[:], c_m2, t_w)
         t_hi, v_j = None, None
+        sc_hi, sh_hi = 1.0 / (16.0 * HI), -0.32 / 16.0 - SHIFT / (16.0 * HI)
         if sends:
             v_j = ts(T.ji[:], T.mis[:, 0:32], 2048.0, None, A.add, None, jt[0], v_s1)
         need("v", v_s1)
@@ -295,69 +328,65 @@ def rank_program(g, core, T, topo):
             for h in range(2):
                 c = 1536 * h + 768 * i
                 if h == 0:
-                    t = ts(T.ext[:, c:c + 768], T.los[:, c:c + 768], 1.0 / (16.0 * HI), -0.32 / 16.0, A.mult, A.add)
+                    t = ts(T.ext[:, c:c + 768], T.los[:, c:c + 768], sc_hi, sh_hi, A.mult, A.add)
                 else:
-                    t = act2(T.ext[:, c:c + 768], T.los[:, c:c + 768], ACT.Copy, -0.32 / 16.0, 1.0 / (16.0 * HI), v_s1)
+                    t = act2(T.ext[:, c:c + 768], T.los[:, c:c + 768], ACT.Copy, sh_hi, sc_hi, v_s1)
                 for q in range(16):
                     t_hi = mm(T.mis[:, c // 16:c // 16 + 48], T.m2[:, 128 * q:128 * q + 128], T.ext[:, c + q:c + 768:16],
                               q == 0, q == 15, t, c_m2, v_j)
-        v_l, v_mk = None, None
+        t_mk = None
         if sends:
             v_q = ts(T.jq[:], T.ji[:], 15, None, A.bitwise_and, None, v_j)
             v_c = ts(T.jc[:], T.ji[:], 4, None, A.logical_shift_right, None, v_j)
-            v_mk = ts(T.mk[:], T.jq[:], T.lane[:], None, A.is_gt, None, v_q, st["lane"])
+            t_mk, n = ts(T.mkt[:, 0:32], T.jq[:], T.lane[:], None, A.is_gt, None, v_q, st["lane"]), 32
+            while n < 1024:
+                t_mk = act(T.mkt[:, n:2 * n], T.mkt[:, 0:n], t_mk)
+                n *= 2
             v = tt(T.jt[:], T.jc[:], T.dq[:], A.mult, v_c, st["lane"])
             need("v", v)
             for b in range(2):
                 v = done("v", V.tensor_reduce(T.cw[:, b:b + 1], T.jt[:, 16 * b:16 * b + 16], AxisListType.X, A.add))
-        v2 = vcopy(T.hii[:], T.mis[:, 0:NC], t_hi)
-        v_d2 = vcopy(T.dig2[:], T.hii[:], v2)
-        if sends:
-            for b in range(2):
-                v_l = ts(T.lst[:, b:64:2], T.hi192[:], T.cw[:, b:b + 1], None, A.add, None, v, c_io)
+        v_d2 = ts(T.dig2[:], T.mis[:, 0:NC], MAGIC, MAGIC, A.add, A.subtract, t_hi)
 
-        def nothing(*a):
-            return None
+        def lists(sc):
+            if sends:
+                for b in range(2):
+                    kt["l"] = ts(T.lst[:, b:64:2], T.hi192[:], T.cw[:, b:b + 1], None, A.add, None, v, c_io)
 
-        v_o2, free, v_ct = sort_pass(T.dig2[:], T.off2, v_d2, free, nothing, nothing, nothing, nothing)
-        t_e = None
+        v_o2, v_ct, _ = sort_pass(T.dig2[:], T.off2, v_d2, [t_kr[0]] * 3, nothing, nothing, lists, nothing)
+        t_e, p, ps_b = None, None, v_o2
         if sends:
-            s_m = None
-            for d in range(32):
-                q = d % 16
-                s_m = act2(T.ms[:, 128 * d:128 * d + 128], T.m2[:, 128 * q:128 * q + 128], ACT.Identity, 0.0, T.mk[:, d:d + 1],
-                           v_mk, c_m2)
-            need("s", v_l, v_ct)
-            s_1 = done("s", S.activation(T.g1[:], T.ct[:].indirect(T.lst[:]), ACT.Copy))
-            s_2 = done("s", S.activation(T.g2[:], T.oh[:].indirect(T.lst[:]), ACT.Copy))
+            need("s", kt["l"], v_ct)
+            s_1 = done("s", S.activation(T.e1[:], T.ct[:].indirect(T.lst[:]), ACT.Copy))
+            s_2 = done("s", S.activation(T.e2[:], T.oh[:].indirect(T.lst[:]), ACT.Copy))
             for q in range(16):
-                mm(T.mis[:, 0:64], T.m2[:, 128 * q:128 * q + 128], T.g1[:, q:1024:16], q == 0, False, s_1, v2)
-            for d in range(32):
-                t_e = mm(T.mis[:, d // 16:64:2], T.ms[:, 128 * d:128 * d + 128], T.g2[:, d:1024:32], False, d == 31, s_2, s_m)
-        need("v", v_o2)
-        v = done("v", V.tensor_copy(T.packed[:].indirect(T.off2[:]), T.los[:]))
-        t_kr = []
-        for h, ps in enumerate((T.psa, T.psb)):
-            t = None
-            for b in range(3):
-                t = row_bank(ps, b, 1536 * h + 512 * b, False, free[h])
-            t_kr.append(act(T.krow[:, 1536 * h:1536 * h + 1536], ps[:], t))
-        need("v", v)
-        v_mx = done("v", V.tensor_tensor_scan(T.srt[:, 8:], T.packed[:], T.packed[:], NEG, A.max, A.max))
+                mm(T.mis[:, 0:64], T.m2[:, 128 * q:128 * q + 128], T.e1[:, q:1024:16], q == 0, False, s_1, v_o2)
+            for b in range(2):
+                mm(T.psb[:, 512 * b:512 * b + 512], T.ident[:], T.e2[:, 512 * b:512 * b + 512], True, False, s_2, ps_b)
+                p = mm(T.psb[:, 512 * b:512 * b + 512], T.ident[:], T.mkt[:, 512 * b:512 * b + 512], False, True, t_mk)
+        need("v", v_o2, g_a)
+        v = done("v", V.tensor_copy(T.packed[:].indirect(T.off2[:, 0:SC_V]), T.los[:, 0:16 * SC_V]))
+        need("s", v_o2, g_b, v_s1)
+        s_w = done("s", S.activation(T.pkb[:].indirect(T.off2[:, SC_V:NC]), T.los[:, 16 * SC_V:], ACT.Silu))
+        if sends:
+            s_3 = ps_b = act2(T.e3[:], T.psb[:, 0:1024], ACT.Relu, -1.0, 1.0, p)
+            for q in range(16):
+                t_e = mm(T.mis[:, 0:64], T.m2[:, 128 * q:128 * q + 128], T.e3[:, q:1024:16], False, q == 15, s_3)
+        need("v", v, s_w)
+        v_mx = done("v", V.tensor_tensor_scan(T.srt[:, 8:], T.packed[:], T.pkb[:], NEG, A.max, A.max))
+        st["mx"] = v_mx
         tl = T["tl%d" % li]
         if sends:
             v_e = ts(T.eoff[:], T.mis[:, 0:64], 2055.0, None, A.add, None, t_e)
             v_t = tt(tl[:], T.srt[:].indirect(T.eoff[:]), T.kc[:], A.subtract, v_mx, v_e, c_kc)
             need("g", v_t)
-            off_chip, on_chip = [], []
-            for d in T.cores[rank + 1:]:
-                (on_chip if d in topo.cores_of(core) else off_chip).append(d)
-            trans, total, used = [], 0, []
+            off_chip = off_chip_of(core)
+            on_chip = [d for d in T.cores[rank + 1:] if d not in off_chip]
+            trans, total = [], 0
             for group in (off_chip, on_chip):
                 if not group:
                     continue
-                eng = [e for e in topo.engines(core, group[0]) if e not in used]
-                used += eng
+                eng = link(core, group[0])
                 total += len(eng)
                 dst = []
                 for d in group:
@@ -378,7 +407,8 @@ def rank_program(g, core, T, topo):
             need("v", v_a, s_a, t_kr[1])
             ys.append(done("v", V.tensor_tensor(dst[:, c:e], T.los[:].indirect(T.off1[:, c // 16:e // 16]), T.krow[:, c:e], A.subtract)))
             if rank == 0:
-                piece_done(c, e, ys[-1])
+                for i, j in ((CUT, STORE), (STORE, S_TOK)) if c else ((0, CUT),):
+                    piece_done(i, j, ys[-1])
         if rank > 0:
             parts, c = [], CUT
             for ps, o in ((T.acc, 0), (T.psa, 1024), (T.psb, 1024)):
@@ -393,7 +423,7 @@ def rank_program(g, core, T, topo):
                 ps = (T.psa, T.psb)[r % 2]
                 for b in range(2):
                     t = mm(ps[:, 512 * b:512 * b + 512], T.ident[:], T["ld%d%d" % (li, r)][:, 512 * b:512 * b + 512], True, True,
-                           ("r%d%d" % (li, r), arrivals(r)), t_kr[r % 2])
+                           ("r%d%d" % (li, r), arrivals(r)), ps_b)
                 merge.append(((T.ta, T.tb)[r % 2], ps, t))
             for nxt, ps, t in merge:
                 v_in = tt(nxt[:], ps[:, 0:1024], tin[:], A.max, t, v_in)
@@ -403,7 +433,9 @@ def rank_program(g, core, T, topo):
             piece_done(0, CUT, tt(out[:, 0:CUT], tin[:].indirect(T.koff[:, 0:CUT // 16]), T.yl[:, 0:CUT], A.max, v_in, ys[1], ko[0]))
             for ps, o, c, n, t in parts:
                 v = tt(out[:, c:c + n], ps[:, o:o + n], T.ext[:, c:c + n], A.max, t, s_t)
-            piece_done(CUT, S_TOK, v)
+                if c + n == STORE:
+                    piece_done(CUT, STORE, v)
+            piece_done(STORE, S_TOK, v)
 
     hk = []
 
@@ -414,14 +446,14 @@ def rank_program(g, core, T, topo):
         hk.append((tok, t))
 
     def store_piece(c, e, tok):
-        dma("y", "dy0" if c else "dy1", T.y[:, c:e], T.yo[:, c:e], tok)
+        dma("y", {0: "dy0", CUT: "dy1"}.get(c, "dy2"), T.y[:, c:e], T.yo[:, c:e], tok)
 
     layer(0, T.xs, t_x, t_k, T.y1, hash_piece)
-    layer(1, T.y1, [hk[0][0], hk[1][0]], hk[1][1], T.yo, store_piece)
+    layer(1, T.y1, [h[0] for h in hk], max(h[1] for h in hk), T.yo, store_piece)
 
     for q in ("v", "s", "p", "g"):
         need("g", ("c" + q, count[q]))
-    for s in ("ds0", "ds1", "dx0", "dx1", "dw", "dy0", "dy1"):
+    for s in ("ds0", "ds1", "dx0", "dx1", "dw", "dy0", "dy1", "dy2"):
         need("g", (s, 16))
     if sends:
         for li in range(2):

@@ -3,59 +3,41 @@ from concourse.mybir import dt, AluOpType, AxisListType, ActivationFunctionType
 
 S_TOK, NC, ND = 3072, 192, 32
 F = NC * ND
-HI = 24576
+UNIT = 510
+HI = 64 * UNIT
 NEG = -1000000.0
 MAGIC = 12582912.0
-ND_V = 20
-MID = (ND_V + ND) // 2
-F_V = NC * ND_V
-FS = F - F_V
+ND_V = (26, 24)
+ND_S = min(ND_V)
+MID = (ND_S + ND) // 2
 EV = 96
-SHIFT = 1024.0
-SC_V = 104
+SHIFT = 26440.0
+SP_V = 112
+PC = 1024
+SC_V = 100
 STORE = 2688
 CUT = 1664
 
+SB = {"bfloat16": {"xs": S_TOK, "y1": S_TOK, "yl": S_TOK, "yo": S_TOK, "ones": 288, "ident": 128, "bm": 128, "bt": 128, "lm": 128,
+                   "i192": 128, "cio": NC, "m2": 2048, "m3": 2048, "wm": 2048, "m2l": 2048, "dl": NC, "sq": NC,
+                   "dgm": 128 * (ND - ND_S), "zero": 3072, "dig1": NC, "dig2": NC, "oh": F + 16, "ct": F + 16, "g1": 16 * EV,
+                   "g2": 16 * EV, "mkt": 32, "e1": 1024, "e2": 1024, "e3": 1024, "ext": S_TOK, "tl0": 1024, "tl1": 1024,
+                   "ld00": 1024, "ld01": 1024, "ld02": 1024, "ld10": 1024, "ld11": 1024, "ld12": 1024, "ta": 1024, "tb": 1024},
+      "float32": {"wc": 1, "lane": 1, "ml": 32, "dq": 32, "hi192": 32, "kc": 1024, "jt": 32, "cw": 2, "packed": S_TOK,
+                  "pkb": S_TOK, "krow": S_TOK, "los": S_TOK, "losb": S_TOK, "srt": S_TOK + 8},
+      "int32": {"pi": 1, "li": 1, "ki": NC, "loi": NC, "keyi": NC, "h16": NC, "ji": 32, "jq": 32, "jc": 32},
+      "float16": {"pk": NC, "msk": ND * EV},
+      "uint16": {"koff": NC, "poff": EV, "off1": NC, "off2": NC, "eoff": 64, "lst": 64}}
 SCRATCH = {
-    "sl_i": ("sbuf", [16, 1536], "int32"), "sl_h": ("sbuf", [16, 1536], "float16"),
-    "xs": ("sbuf", [128, S_TOK], "bfloat16"), "y1": ("sbuf", [128, S_TOK], "bfloat16"),
-    "yl": ("sbuf", [128, S_TOK], "bfloat16"), "yo": ("sbuf", [128, S_TOK], "bfloat16"),
-    "wc": ("sbuf", [128, 1], "float32"),
-    "ones": ("sbuf", [128, 288], "bfloat16"), "wd": ("sbuf", [16, 288], "bfloat16"),
-    "ident": ("sbuf", [128, 128], "bfloat16"), "bm": ("sbuf", [128, 128], "bfloat16"), "bt": ("sbuf", [128, 128], "bfloat16"),
-    "lm": ("sbuf", [128, 128], "bfloat16"), "um": ("sbuf", [128, 128], "bfloat16"),
-    "i192": ("sbuf", [128, 128], "bfloat16"), "cio": ("sbuf", [128, NC], "bfloat16"),
-    "m2": ("sbuf", [128, 2048], "bfloat16"), "m3": ("sbuf", [128, 2048], "bfloat16"), "wm": ("sbuf", [128, 2048], "bfloat16"),
-    "m2l": ("sbuf", [128, 2048], "bfloat16"),
-    "dl": ("sbuf", [128, NC], "bfloat16"), "sq": ("sbuf", [128, NC], "bfloat16"),
-    "dgm": ("sbuf", [128, 128 * (ND - ND_V)], "bfloat16"), "e2r": ("sbuf", [1, 1536], "bfloat16"),
-    "pi": ("sbuf", [128, 1], "int32"), "li": ("sbuf", [128, 1], "int32"), "lane": ("sbuf", [128, 1], "float32"),
-    "ml": ("sbuf", [128, 32], "float32"), "dq": ("sbuf", [128, 32], "float32"), "hi192": ("sbuf", [128, 32], "float32"),
-    "kc": ("sbuf", [128, 1024], "float32"), "zero": ("sbuf", [128, 3072], "bfloat16"),
-    "ki": ("sbuf", [128, NC], "int32"), "loi": ("sbuf", [128, NC], "int32"),
-    "keyi": ("sbuf", [128, NC], "int32"), "h16": ("sbuf", [128, NC], "int32"), "pk": ("sbuf", [128, NC], "float16"),
-    "dig1": ("sbuf", [128, NC], "bfloat16"), "dig2": ("sbuf", [128, NC], "bfloat16"), "koff": ("sbuf", [128, NC], "uint16"),
-    "poff": ("sbuf", [128, EV], "uint16"),
-    "off1": ("sbuf", [128, NC], "uint16"), "off2": ("sbuf", [128, NC], "uint16"),
-    "eoff": ("sbuf", [128, 64], "uint16"), "lst": ("sbuf", [128, 64], "uint16"),
-    "oh": ("sbuf", [128, F + 16], "bfloat16"), "ct": ("sbuf", [128, F + 16], "bfloat16"),
-    "msk": ("sbuf", [128, ND * EV], "float16"),
-    "g1": ("sbuf", [128, 16 * EV], "bfloat16"), "g2": ("sbuf", [128, 16 * EV], "bfloat16"),
-    "ji": ("sbuf", [128, 32], "int32"), "jq": ("sbuf", [128, 32], "int32"), "jc": ("sbuf", [128, 32], "int32"),
-    "jt": ("sbuf", [128, 32], "float32"), "cw": ("sbuf", [128, 2], "float32"), "mkt": ("sbuf", [128, 1024], "bfloat16"),
-    "e1": ("sbuf", [128, 1024], "bfloat16"), "e2": ("sbuf", [128, 1024], "bfloat16"), "e3": ("sbuf", [128, 1024], "bfloat16"),
-    "packed": ("sbuf", [128, S_TOK], "float32"), "pkb": ("sbuf", [128, S_TOK], "float32"),
-    "krow": ("sbuf", [128, S_TOK], "float32"),
-    "los": ("sbuf", [128, S_TOK], "float32"), "ext": ("sbuf", [128, S_TOK], "bfloat16"),
-    "srt": ("sbuf", [128, S_TOK + 8], "float32"),
-    "tl0": ("sbuf", [128, 1024], "bfloat16"), "tl1": ("sbuf", [128, 1024], "bfloat16"),
-    "ld00": ("sbuf", [128, 1024], "bfloat16"), "ld01": ("sbuf", [128, 1024], "bfloat16"), "ld02": ("sbuf", [128, 1024], "bfloat16"),
-    "ld10": ("sbuf", [128, 1024], "bfloat16"), "ld11": ("sbuf", [128, 1024], "bfloat16"), "ld12": ("sbuf", [128, 1024], "bfloat16"),
-    "ta": ("sbuf", [128, 1024], "bfloat16"), "tb": ("sbuf", [128, 1024], "bfloat16"),
+    "sl_i": ("sbuf", [16, 1536], "int32"), "sl_h": ("sbuf", [16, 1536], "float16"), "wd": ("sbuf", [16, 288], "bfloat16"),
+    "e2r": ("sbuf", [1, 1536], "bfloat16"),
     "psa": ("psum", [128, 1536], "float32"), "psb": ("psum", [128, 1536], "float32"),
     "acc": ("psum", [128, 512], "float32"), "mis": ("psum", [128, 512], "float32"),
 }
-SEMAPHORES = (["cv", "cs", "cp", "cg", "dx0", "dx1", "ds0", "ds1", "dw", "dy0", "dy1", "dy2", "lo0", "lo1"]
+for _t in SB:
+    for _n in SB[_t]:
+        SCRATCH[_n] = ("sbuf", [128, SB[_t][_n]], _t)
+SEMAPHORES = (["cv", "cs", "cp", "cg", "dx0", "dx1", "ds0", "ds1", "dw", "dz", "da0", "da1", "dy0", "dy1", "dy2", "lo0", "lo1"]
               + ["r%d%d" % (a, b) for a in range(2) for b in range(3)])
 
 
@@ -129,9 +111,8 @@ def rank_program(g, core, T, topo):
     t_w = dma("y", "dw", T.wc[:], T.w[:])
 
     f_one = fill(T.ones[:], 1.0)
-    f_m3 = fill(T.m3[:], 512.0)
     f_m2 = fill(T.m2[:], 0.0)
-    f_m2l = fill(T.m2l[:], 0.0)
+    f_m3 = fill(T.m3[:], float(UNIT))
 
     def sel(out, in_, pattern, op, base, cm, *deps):
         need("g", *deps)
@@ -142,22 +123,21 @@ def rank_program(g, core, T, topo):
     t0 = sel(T.bt[:], T.ones[:, 0:128], [[-16, 8], [0, 16]], A.is_ge, 0, 1)
     c_b = sel(T.bm[:], T.bt[:], [[16, 8], [0, 16]], A.is_ge, 15, -1, t0)
     c_lm = sel(T.lm[:], T.bm[:], [[1, 128]], A.is_gt, 0, -1, c_b)
-    c_um = sel(T.um[:], T.bm[:], [[-1, 128]], A.is_ge, 0, 1)
     c_m3 = sel(T.m3[:], T.m3[:], [[-1, 16], [-16, 8], [0, 16]], A.is_equal, 0, 1, f_m3)
     c_cio = done("g", g.iota(T.cio[:], [[1, NC]], 0, 0, allow_small_or_imprecise_dtypes=True))
     done("g", g.iota(T.pi[:], [[0, 1]], 0, 1))
     done("g", g.iota(T.ml[:], [[0, 2], [1, 16]], 0, 0, allow_small_or_imprecise_dtypes=True))
     c_io = done("g", g.iota(T.hi192[:], [[NC, 32]], 0, 0, allow_small_or_imprecise_dtypes=True))
-    c_kc = done("g", g.iota(T.kc[:], [[HI, 32], [512, 32]], int(SHIFT), 0, allow_small_or_imprecise_dtypes=True))
-    c_m2 = None
-    for q in range(16):
-        act(T.m2[:, 128 * q + q:128 * q + 128:16], T.bm[:, q:128:16], c_b, f_m2)
-    for q in range(16):
-        c_m2 = act(T.m2l[:, 128 * q + q:128 * q + 128:16], T.lm[:, q:128:16], c_lm, f_m2l)
+    f_m2l = act(T.m2l[:], T.m2[:], f_m2)
     c_192 = act2(T.i192[:], T.ident[:], ACT.Silu, 0.0, 192.0, c_id)
     c_dg = None
-    for i in range(ND - ND_V):
-        c_dg = act2(T.dgm[:, 128 * i:128 * i + 128], T.ident[:], ACT.Copy, 0.0, -2.0 * (ND_V + i - MID), c_id)
+    for i in range(ND - ND_S):
+        c_dg = act2(T.dgm[:, 128 * i:128 * i + 128], T.ident[:], ACT.Copy, 0.0, -2.0 * (ND_S + i - MID), c_id)
+    c_m2 = None
+    for q in range(16):
+        act(T.m2[:, 128 * q + q:128 * q + 128:16], T.bm[:, q:128:16], c_b, f_m2, f_m2l)
+    for q in range(16):
+        c_m2 = act(T.m2l[:, 128 * q + q:128 * q + 128:16], T.lm[:, q:128:16], c_lm, f_m2l)
 
     t_k = None
     for i in range(2):
@@ -166,19 +146,24 @@ def rank_program(g, core, T, topo):
             for q in range(16):
                 o, c = 128 * h + 15 - q, 96 * h + 48 * i
                 t_k = mm(T.mis[:, c:c + 48], T.wd[:, o:o + 128], T.sl_h[:, 768 * i + q:768 * i + 768:16], q == 0, q == 15, v0, c_wd)
+    f_zero = fill(T.zero[:], 0.0)
     fill(T.ct[:, 0:1], -128.0)
-    fill(T.zero[:], 0.0)
     fill(T.ct[:, F + 1:F + 16], 0.0)
     fill(T.oh[:, F:F + 16], 0.0)
     f_end = fill(T.srt[:, 0:8], NEG)
-    for e in range(1, MID - ND_V + 1):
+    for e in range(1, max(MID - ND_S, ND - 1 - MID) + 1):
         f_end = fill(T.e2r[:, 128 * e:128 * e + 128], float(e * e))
 
-    def low(buf, *deps):
+    def low(buf, *deps, c=int(NEG)):
         need("g", *deps)
-        return done("g", g.iota(buf[:], [[0, S_TOK]], int(NEG), 0, allow_small_or_imprecise_dtypes=True))
+        return done("g", g.iota(buf[:], [[0, S_TOK]], c, 0, allow_small_or_imprecise_dtypes=True))
 
-    st = {"lane": None, "wm": None, "mx": None}
+    need("g", f_zero)
+    g.dma_start(T.losb[:], T.zero[:]).then_inc(T.sem["dz"], 16)
+    z_a = low(T.los, c=0)
+    c_kc = done("g", g.iota(T.kc[:], [[HI, 32], [UNIT, 32]], int(SHIFT), 0, allow_small_or_imprecise_dtypes=True))
+
+    st = {"lane": None, "wm": None, "mx": None, "za": z_a, "zb": ("dz", 16)}
 
     def off_chip_of(src):
         r = T.rank_of(src)
@@ -191,61 +176,77 @@ def rank_program(g, core, T, topo):
             return eng
         if offs:
             eng = [e for e in eng if e not in topo.engines(src, offs[0])]
-        return eng[:len(eng) // 2]
+        return eng[::2]
 
     def arrivals(r):
         return len(link(T.cores[r], core))
 
-    def sort_pass(dig, off, dep, ps_free, early_v, mid, fillers, late):
+    def nothing(*a):
+        return None
+
+    def sort_pass(nd, dig, off, dep, ps_free, early_v, inter, hook2, hook1, fillers, late):
         mm(T.acc[:, 256:256 + EV], T.i192[:], dig[:, 1:NC:2], True, False, dep, c_192)
         t_po = mm(T.acc[:, 256:256 + EV], T.ident[:], T.cio[:, 1:NC:2], False, True, c_id, c_cio)
         t_dl = act2(T.dl[:], dig, ACT.Copy, -float(MID), 1.0, dep)
         t_sq = act2(T.sq[:], dig, ACT.Square, -float(MID), 1.0, dep)
-        n = FS // 512 + (FS % 512 > 0)
-        relu, s_oh = list(ps_free), None
-        for b in range(n):
-            o, w, c, t = 512 * (b % 3), min(512, FS - 512 * b), 512 * b, None
-            while c < 512 * b + w:
-                i = c // NC
-                m = min(NC * (i + 1), 512 * b + w)
-                e = ND_V + i - MID
-                z, k = T.psa[:, o + c - 512 * b:o + m - 512 * b], c - NC * i
-                if e:
-                    mm(z, T.dgm[:, 128 * i:128 * i + 128], T.dl[:, k:k + m - c], True, False, t_dl, c_dg, relu[b % 3])
-                    mm(z, T.e2r[:, 128 * abs(e):128 * abs(e) + 128], T.ones[0:1, 0:m - c], False, False, f_end)
-                t = mm(z, T.ident[:], T.sq[:, k:k + m - c], e == 0, True, t_sq, c_id, relu[b % 3])
-                c = m
-            s_oh = act2(T.oh[:, F_V + 512 * b:F_V + 512 * b + w], T.psa[:, o:o + w], ACT.Relu, 1.0, -1.0, t, f_end)
-            relu[b % 3] = s_oh
         v_oh, v_po = None, None
-        for d in range(ND_V):
+        for d in range(nd):
             if d == 4:
                 early_v()
             if d == 12:
                 v_po = vcopy(T.poff[:], T.acc[:, 256:256 + EV], t_po)
             v_oh = ts(T.oh[:, NC * d:NC * d + NC], dig, float(d), None, A.is_equal, None, dep)
-        mid()
+        f_v, f_s = NC * nd, F - NC * nd
+        n = f_s // 512 + (f_s % 512 > 0)
+        relu, s_oh = list(ps_free), None
+        for b in range(n):
+            o, w, c, t = 512 * (b % 3), min(512, f_s - 512 * b), 512 * b, None
+            while c < 512 * b + w:
+                i = c // NC
+                m = min(NC * (i + 1), 512 * b + w)
+                e, j = nd + i - MID, nd + i - ND_S
+                z, k = T.psa[:, o + c - 512 * b:o + m - 512 * b], c - NC * i
+                if e:
+                    mm(z, T.dgm[:, 128 * j:128 * j + 128], T.dl[:, k:k + m - c], True, False, t_dl, c_dg, relu[b % 3])
+                    mm(z, T.e2r[:, 128 * abs(e):128 * abs(e) + 128], T.ones[0:1, 0:m - c], False, False, f_end)
+                t = mm(z, T.ident[:], T.sq[:, k:k + m - c], e == 0, True, t_sq, c_id, relu[b % 3])
+                c = m
+            if b == n - 1:
+                inter()
+            s_oh = act2(T.oh[:, f_v + 512 * b:f_v + 512 * b + w], T.psa[:, o:o + w], ACT.Relu, 1.0, -1.0, t, f_end)
+            relu[b % 3] = s_oh
         sc, c, tok = None, 0, {}
         while c < F:
-            w = min(3072, (F_V if c < F_V else F) - c)
-            need("v", v_oh, sc, s_oh if c >= F_V else None)
+            w = min(3072, (f_v if c < f_v else F) - c)
+            need("v", v_oh, sc, s_oh if c >= f_v else None)
             init = -128.0 if c == 0 else T.ct[:, c:c + 1]
             sc = done("v", V.tensor_tensor_scan(T.ct[:, c + 1:c + w + 1], T.oh[:, c:c + w], T.zero[:, 0:w], init, A.add, A.add))
             c += w
             tok[c] = sc
+        bank = list(relu)
+
+        def early(b):
+            z, a = T.psa[:, 512 * (b % 3):512 * (b % 3) + 512], 1024 * b
+            mm(z, T.lm[:], T.oh[:, a:a + 1024:2], True, False, v_oh, s_oh if a + 1024 > f_v else None, c_lm, bank[b % 3])
+
+        for b in range(3):
+            early(b)
+        hook2()
         need("s", v_oh, s_oh, v_po)
         s_2 = done("s", S.activation(T.g2[:], T.oh[:].indirect(T.poff[:]), ACT.Copy))
         need("s", sc)
         s_1 = done("s", S.activation(T.g1[:], T.ct[:].indirect(T.poff[:]), ACT.Copy))
-        bank, red, d, t = list(relu), [], 0, None
+        hook1()
+        red, d, t = [], 0, None
         for b in range(6):
             z, a = T.psa[:, 512 * (b % 3):512 * (b % 3) + 512], 1024 * b
-            t = tok[min(k for k in tok if k >= min(a + 1025, F))]
-            mm(z, T.lm[:], T.ct[:, a + 1:a + 1025:2], True, False, t, c_lm, bank[b % 3])
-            t = mm(z, T.um[:], T.ct[:, a:a + 1024:2], False, True, c_um)
+            if b > 2:
+                early(b)
+            t = tok[min(k for k in tok if k >= a + 1024)]
+            t = mm(z, T.bm[:], T.ct[:, a:a + 1024:2], False, True, t, c_b)
             bank[b % 3] = tt(T.msk[:, 512 * b:512 * b + 512], z, T.oh[:, a:a + 1024:2], A.mult, t)
             red.append(bank[b % 3])
-            if b == 3:
+            if b == 2:
                 fillers(sc)
                 for q in range(16):
                     mm(T.mis[:, 256:256 + EV], T.m2l[:, 128 * q:128 * q + 128], T.g2[:, q:16 * EV:16], q == 0, False, s_2, c_m2)
@@ -267,11 +268,11 @@ def rank_program(g, core, T, topo):
         v = vcopy(T.ki[:], T.mis[:, 0:NC], key_tok)
         v_lo = ts(T.loi[:], T.ki[:], 31, None, A.bitwise_and, None, v)
         v_d1 = vcopy(T.dig1[:], T.loi[:], v_lo)
-        kt, t_p, t_kr, jt, pb, ko = {}, [], [], [None], [], []
+        kt, t_p, jt, pb, ko = {}, [], [None], [], []
 
         def pack_keys():
             a = ts(T.keyi[:], T.ki[:], 1023, None, A.bitwise_and, None, v)
-            b = ts(T.h16[:], T.ki[:], 992, 1, A.bitwise_and, A.logical_shift_right, v)
+            b = ts(T.h16[:], T.ki[:], 992, None, A.bitwise_and, None, v)
             kt["pk"] = tt(T.pk[:], T.keyi[:], T.h16[:], A.add, a, b)
             kt["key"] = a
 
@@ -284,12 +285,29 @@ def rank_program(g, core, T, topo):
                        not with_src, q == 15 or not with_src, kt["pk"], c_m3, *deps)
             return t
 
-        def packs(h, free):
-            for b in range(3):
-                pb.append(row_bank(T.psb, b, 1536 * h + 512 * b, True, free[b]))
-            for b in range(3):
-                t_p.append(act2(T.packed[:, 1536 * h + 512 * b:1536 * h + 512 * b + 512], T.psb[:, 512 * b:512 * b + 512], ACT.Copy,
-                                SHIFT, 1.0, pb[3 * h + b], st["mx"]))
+        def pack_p(i, free):
+            pb.append(row_bank(T.psb, i % 3, 512 * i, True, free))
+
+        def pack_s(i):
+            t_p.append(act2(T.packed[:, 512 * i:512 * i + 512], T.psb[:, 512 * (i % 3):512 * (i % 3) + 512], ACT.Copy, SHIFT, 1.0,
+                            pb[i], st["mx"]))
+
+        def packs_x():
+            for i in range(3):
+                pack_p(i, None)
+
+        def packs_y():
+            for i in range(3):
+                pack_s(i)
+            pack_p(3, t_p[0])
+
+        def packs_z():
+            pack_s(3)
+
+        def packs_l():
+            for i in (4, 5):
+                pack_p(i, t_p[i - 3])
+                pack_s(i)
 
         def fillers(sc):
             if sends:
@@ -300,61 +318,59 @@ def rank_program(g, core, T, topo):
                 a = vcopy(T.lane[:], T.li[:], a)
                 st["lane"] = ts(T.dq[:], T.ml[:], T.lane[:], None, A.is_equal, None, a)
 
-        def nothing(*a):
-            return None
-
-        v_o1, _, psa_t = sort_pass(T.dig1[:], T.off1, v_d1, [None] * 3, pack_keys, lambda: packs(0, [None] * 3), fillers,
-                                   lambda: packs(1, t_p))
-        v = None
-        for h in range(2):
-            need("v", v_o1, t_p[3 * h + 2], v)
-            v = done("v", V.tensor_copy(T.los[:].indirect(T.off1[:, 96 * h:96 * h + 96]), T.packed[:, 1536 * h:1536 * h + 1536]))
-        v_s1 = v
         g_b = low(T.pkb, st["mx"])
-        g_a = low(T.packed, v_s1)
-        for h, ps in enumerate((T.psa, T.psb)):
-            t = None
+        v_o1, _, psa_t = sort_pass(ND_V[0], T.dig1[:], T.off1, v_d1, [None] * 3, pack_keys, packs_x, packs_y, packs_z, fillers,
+                                   packs_l)
+        need("v", v_o1, st["za"], *t_p[:(16 * SP_V + 511) // 512])
+        v_s1 = done("v", V.tensor_copy(T.los[:].indirect(T.off1[:, 0:SP_V]), T.packed[:, 0:16 * SP_V]))
+        need("s", v_o1, st["zb"], *t_p)
+        s_s1 = done("s", S.activation(T.losb[:].indirect(T.off1[:, SP_V:NC]), T.packed[:, 16 * SP_V:], ACT.Silu))
+        pk_r = [None, None]
+
+        def key_mm(h, *deps):
             for b in range(3):
-                t = row_bank(ps, b, 1536 * h + 512 * b, False, psa_t[b] if h == 0 else t_p[3 + b])
-            t_kr.append(act2(T.krow[:, 1536 * h:1536 * h + 1536], ps[:], ACT.Copy, SHIFT, 1.0, t))
-        if st["wm"] is None:
-            st["wm"] = act2(T.wm[:], T.m2[:], ACT.Copy, 0.0, T.wc[:], c_m2, t_w)
-        t_hi, v_j = None, None
-        sc_hi, sh_hi = 1.0 / (16.0 * HI), -0.32 / 16.0 - SHIFT / (16.0 * HI)
+                pk_r[h] = row_bank((T.psa, T.psb)[h], b, 1536 * h + 512 * b, False, *deps)
+
+        def key_rows(h):
+            return act2(T.krow[:, 1536 * h:1536 * h + 1536], (T.psa, T.psb)[h][:], ACT.Copy, SHIFT, 1.0, pk_r[h])
+
+        key_mm(1, *t_p[3:6])
+        t_hi, v_j, sc_hi = None, None, 1.0 / (16.0 * HI)
         if sends:
-            v_j = ts(T.ji[:], T.mis[:, 0:32], 2048.0, None, A.add, None, jt[0], v_s1)
+            v_j = ts(T.ji[:], T.mis[:, 0:32], 2048.0, None, A.add, None, jt[0], v_o1)
         need("v", v_s1)
-        for i in range(2):
-            for h in range(2):
-                c = 1536 * h + 768 * i
-                if h == 0:
-                    t = ts(T.ext[:, c:c + 768], T.los[:, c:c + 768], sc_hi, sh_hi, A.mult, A.add)
-                else:
-                    t = act2(T.ext[:, c:c + 768], T.los[:, c:c + 768], ACT.Copy, sh_hi, sc_hi, v_s1)
+        need("s", s_s1)
+        t_da = ("da%d" % li, 16)
+        for c in range(S_TOK - PC, -1, -PC):
+            e_a = ts(T.ext[:, c:c + PC], T.los[:, c:c + PC], sc_hi, None, A.mult, None)
+            e_b = act2(T.yo[:, c:c + PC], T.losb[:, c:c + PC], ACT.Copy, 0.0, sc_hi)
+            if c <= 16 * SC_V < c + PC:
+                need("g", e_a, s_s1)
+                g.dma_start(T.los[:, 16 * SC_V:], T.losb[:, 16 * SC_V:], accum_op=A.add).then_inc(T.sem[t_da[0]], 16)
+            for last, x, t in ((False, T.ext, e_a), (True, T.yo, e_b)):
                 for q in range(16):
-                    t_hi = mm(T.mis[:, c // 16:c // 16 + 48], T.m2[:, 128 * q:128 * q + 128], T.ext[:, c + q:c + 768:16],
-                              q == 0, q == 15, t, c_m2, v_j)
+                    t_hi = mm(T.mis[:, c // 16:(c + PC) // 16], T.m2[:, 128 * q:128 * q + 128], x[:, c + q:c + PC:16],
+                              q == 0 and not last, q == 15 and last, t, c_m2, v_j)
+        g_a = low(T.packed, v_s1, s_s1)
+        t_kr = [None, None]
         t_mk = None
         if sends:
             v_q = ts(T.jq[:], T.ji[:], 15, None, A.bitwise_and, None, v_j)
             v_c = ts(T.jc[:], T.ji[:], 4, None, A.logical_shift_right, None, v_j)
-            t_mk, n = ts(T.mkt[:, 0:32], T.jq[:], T.lane[:], None, A.is_gt, None, v_q, st["lane"]), 32
-            while n < 1024:
-                t_mk = act(T.mkt[:, n:2 * n], T.mkt[:, 0:n], t_mk)
-                n *= 2
+            t_mk = ts(T.mkt[:], T.jq[:], T.lane[:], None, A.is_gt, None, v_q, st["lane"])
             v = tt(T.jt[:], T.jc[:], T.dq[:], A.mult, v_c, st["lane"])
             need("v", v)
             for b in range(2):
                 v = done("v", V.tensor_reduce(T.cw[:, b:b + 1], T.jt[:, 16 * b:16 * b + 16], AxisListType.X, A.add))
-        v_d2 = ts(T.dig2[:], T.mis[:, 0:NC], MAGIC, MAGIC, A.add, A.subtract, t_hi)
+        v_d2 = ts(T.dig2[:], T.mis[:, 0:NC], MAGIC, MAGIC + 1.0, A.add, A.subtract, t_hi)
 
         def lists(sc):
             if sends:
                 for b in range(2):
                     kt["l"] = ts(T.lst[:, b:64:2], T.hi192[:], T.cw[:, b:b + 1], None, A.add, None, v, c_io)
 
-        v_o2, v_ct, _ = sort_pass(T.dig2[:], T.off2, v_d2, [t_kr[0]] * 3, nothing, nothing, lists, nothing)
-        t_e, p, ps_b = None, None, v_o2
+        v_o2, v_ct, _ = sort_pass(ND_V[1], T.dig2[:], T.off2, v_d2, [None] * 3, nothing, nothing, nothing, nothing, lists, nothing)
+        t_e, p, ps_a = None, None, v_o2
         if sends:
             need("s", kt["l"], v_ct)
             s_1 = done("s", S.activation(T.e1[:], T.ct[:].indirect(T.lst[:]), ACT.Copy))
@@ -362,16 +378,20 @@ def rank_program(g, core, T, topo):
             for q in range(16):
                 mm(T.mis[:, 0:64], T.m2[:, 128 * q:128 * q + 128], T.e1[:, q:1024:16], q == 0, False, s_1, v_o2)
             for b in range(2):
-                mm(T.psb[:, 512 * b:512 * b + 512], T.ident[:], T.e2[:, 512 * b:512 * b + 512], True, False, s_2, ps_b)
-                p = mm(T.psb[:, 512 * b:512 * b + 512], T.ident[:], T.mkt[:, 512 * b:512 * b + 512], False, True, t_mk)
-        need("v", v_o2, g_a)
-        v = done("v", V.tensor_copy(T.packed[:].indirect(T.off2[:, 0:SC_V]), T.los[:, 0:16 * SC_V]))
-        need("s", v_o2, g_b, v_s1)
+                mm(T.psa[:, 512 * b:512 * b + 512], T.ident[:], T.e2[:, 512 * b:512 * b + 512], True, False, s_2, v_o2)
+                for i in range(16):
+                    c = 512 * b + 32 * i
+                    p = mm(T.psa[:, c:c + 32], T.ident[:], T.mkt[:], False, i == 15, t_mk)
+        need("v", v_o2, g_a, v_s1, s_s1)
+        v = done("v", V.tensor_tensor(T.packed[:].indirect(T.off2[:, 0:SC_V]), T.los[:, 0:16 * SC_V], T.losb[:, 0:16 * SC_V], A.add))
+        need("s", v_o2, g_b, t_da)
         s_w = done("s", S.activation(T.pkb[:].indirect(T.off2[:, SC_V:NC]), T.los[:, 16 * SC_V:], ACT.Silu))
         if sends:
-            s_3 = ps_b = act2(T.e3[:], T.psb[:, 0:1024], ACT.Relu, -1.0, 1.0, p)
+            s_3 = ps_a = act2(T.e3[:], T.psa[:, 0:1024], ACT.Relu, -1.0, 1.0, p)
             for q in range(16):
                 t_e = mm(T.mis[:, 0:64], T.m2[:, 128 * q:128 * q + 128], T.e3[:, q:1024:16], False, q == 15, s_3)
+        key_mm(0, ps_a)
+        t_kr[1] = key_rows(1)
         need("v", v, s_w)
         v_mx = done("v", V.tensor_tensor_scan(T.srt[:, 8:], T.packed[:], T.pkb[:], NEG, A.max, A.max))
         st["mx"] = v_mx
@@ -382,38 +402,43 @@ def rank_program(g, core, T, topo):
             need("g", v_t)
             off_chip = off_chip_of(core)
             on_chip = [d for d in T.cores[rank + 1:] if d not in off_chip]
-            trans, total = [], 0
-            for group in (off_chip, on_chip):
-                if not group:
-                    continue
-                eng = link(core, group[0])
-                total += len(eng)
-                dst = []
+            total = 0
+            for group in [c for c in (off_chip[:1], on_chip + off_chip[1:]) if c]:
+                trans = []
                 for d in group:
+                    eng = link(core, d)
+                    total += len(eng)
                     rid, pid = topo.addr(d, core)
-                    dst.append(DstId(rid=rid, pnc=pid))
-                trans.append(RemoteDMATransfer(dst_ids=dst, dma_engine_mask=mask_of(eng), remote_sem=T.sem["r%d%d" % (li, rank)],
-                                               srcs=[tl[:]], dsts=[T["ld%d%d" % (li, rank)][:] for d in group]))
-            g.remote_dma_fused(trans, local_sem=T.sem["lo%d" % li])
+                    trans.append(RemoteDMATransfer(dst_ids=[DstId(rid=rid, pnc=pid)], dma_engine_mask=mask_of(eng),
+                                                   remote_sem=T.sem["r%d%d" % (li, rank)], srcs=[tl[:]],
+                                                   dsts=[T["ld%d%d" % (li, rank)][:]]))
+                g.remote_dma_fused(trans, local_sem=T.sem["lo%d" % li])
             st["lo%d" % li] = total
+        if li == 0:
+            st["zb"] = low(T.losb, v_mx, c=0)
         a = 64 if sends else 96
         need("v", v_mx)
         v_a = done("v", V.tensor_copy(T.los[:, 0:16 * a], T.srt[:, 8:].indirect(T.off2[:, 0:a])))
         need("s", v_mx)
         s_a = done("s", S.activation(T.los[:, 16 * a:], T.srt[:, 8:].indirect(T.off2[:, a:NC]), ACT.Copy))
+        t_kr[0] = key_rows(0)
+        if st["wm"] is None:
+            st["wm"] = act2(T.wm[:], T.m2[:], ACT.Copy, 0.0, T.wc[:], c_m2, t_w)
         dst = T.yl if rank > 0 else out
         ys = []
         for c, e in ((CUT, S_TOK), (0, CUT)):
-            need("v", v_a, s_a, t_kr[1])
+            need("v", v_a, s_a, t_kr[1], t_kr[0] if c < 1536 else None)
             ys.append(done("v", V.tensor_tensor(dst[:, c:e], T.los[:].indirect(T.off1[:, c // 16:e // 16]), T.krow[:, c:e], A.subtract)))
             if rank == 0:
                 for i, j in ((CUT, STORE), (STORE, S_TOK)) if c else ((0, CUT),):
                     piece_done(i, j, ys[-1])
+        if li == 0:
+            st["za"] = low(T.los, *ys, c=0)
         if rank > 0:
             parts, c = [], CUT
             for ps, o in ((T.acc, 0), (T.psa, 1024), (T.psb, 1024)):
                 n = min(512, S_TOK - c)
-                t = mm(ps[:, o:o + n], T.ident[:], T.yl[:, c:c + n], True, True, ys[0], t_kr[1])
+                t = mm(ps[:, o:o + n], T.ident[:], T.yl[:, c:c + n], True, True, ys[0], t_kr[0], t_kr[1])
                 parts.append((ps, o, c, n, t))
                 c += n
             tin = T["ld%d0" % li]
@@ -423,7 +448,7 @@ def rank_program(g, core, T, topo):
                 ps = (T.psa, T.psb)[r % 2]
                 for b in range(2):
                     t = mm(ps[:, 512 * b:512 * b + 512], T.ident[:], T["ld%d%d" % (li, r)][:, 512 * b:512 * b + 512], True, True,
-                           ("r%d%d" % (li, r), arrivals(r)), ps_b)
+                           ("r%d%d" % (li, r), arrivals(r)), ps_a, t_kr[0])
                 merge.append(((T.ta, T.tb)[r % 2], ps, t))
             for nxt, ps, t in merge:
                 v_in = tt(nxt[:], ps[:, 0:1024], tin[:], A.max, t, v_in)
@@ -453,7 +478,7 @@ def rank_program(g, core, T, topo):
 
     for q in ("v", "s", "p", "g"):
         need("g", ("c" + q, count[q]))
-    for s in ("ds0", "ds1", "dx0", "dx1", "dw", "dy0", "dy1", "dy2"):
+    for s in ("ds0", "ds1", "dx0", "dx1", "dw", "dz", "da0", "da1", "dy0", "dy1", "dy2"):
         need("g", (s, 16))
     if sends:
         for li in range(2):

from concourse.bass import DstId, RemoteDMATransfer
from concourse.mybir import dt, AluOpType, AxisListType, ActivationFunctionType

S_TOK, NC, ND = 3072, 192, 32
F = NC * ND
UNIT = 510
HI = 64 * UNIT
NEG = -1000000.0
MAGIC = 12582912.0
ND_V = (26, 24)
ND_S = min(ND_V)
MID = (ND_S + ND) // 2
EV = 96
SHIFT = 26440.0
SP_V = 112
PC = 1024
SC_V = 100
STORE = 2688
CUT = 1664

SB = {"bfloat16": {"xs": S_TOK, "y1": S_TOK, "yl": S_TOK, "yo": S_TOK, "ones": 288, "ident": 128, "bm": 128, "bt": 128, "lm": 128,
                   "i192": 128, "cio": NC, "m2": 2048, "m3": 2048, "wm": 2048, "m2l": 2048, "dl": NC, "sq": NC,
                   "dgm": 128 * (ND - ND_S), "zero": 3072, "dig1": NC, "dig2": NC, "oh": F + 16, "ct": F + 16, "g1": 16 * EV,
                   "g2": 16 * EV, "mkt": 32, "e1": 1024, "e2": 1024, "e3": 1024, "ext": S_TOK, "tl0": 1024, "tl1": 1024,
                   "ld00": 1024, "ld01": 1024, "ld02": 1024, "ld10": 1024, "ld11": 1024, "ld12": 1024, "ta": 1024, "tb": 1024},
      "float32": {"wc": 1, "lane": 1, "ml": 32, "dq": 32, "hi192": 32, "kc": 1024, "jt": 32, "cw": 2, "packed": S_TOK,
                  "pkb": S_TOK, "krow": S_TOK, "los": S_TOK, "losb": S_TOK, "srt": S_TOK + 8},
      "int32": {"pi": 1, "li": 1, "ki": NC, "loi": NC, "keyi": NC, "h16": NC, "ji": 32, "jq": 32, "jc": 32},
      "float16": {"pk": NC, "msk": ND * EV},
      "uint16": {"koff": NC, "poff": EV, "off1": NC, "off2": NC, "eoff": 64, "lst": 64}}
SCRATCH = {
    "sl_i": ("sbuf", [16, 1536], "int32"), "sl_h": ("sbuf", [16, 1536], "float16"), "wd": ("sbuf", [16, 288], "bfloat16"),
    "e2r": ("sbuf", [1, 1536], "bfloat16"),
    "psa": ("psum", [128, 1536], "float32"), "psb": ("psum", [128, 1536], "float32"),
    "acc": ("psum", [128, 512], "float32"), "mis": ("psum", [128, 512], "float32"),
}
for _t in SB:
    for _n in SB[_t]:
        SCRATCH[_n] = ("sbuf", [128, SB[_t][_n]], _t)
SEMAPHORES = (["cv", "cs", "cp", "cg", "dx0", "dx1", "ds0", "ds1", "dw", "dz", "da0", "da1", "dy0", "dy1", "dy2", "lo0", "lo1"]
              + ["r%d%d" % (a, b) for a in range(2) for b in range(3)])


def mask_of(engines):
    return sum(1 << e for e in engines)


def rank_program(g, core, T, topo):
    rank = T.rank_of(core)
    if rank is None:
        return
    A, ACT = AluOpType, ActivationFunctionType
    V, S, P, Y = g.vector, g.scalar, g.tensor, g.sync
    queue = {"v": V, "s": S, "p": P, "g": g, "y": Y}
    count = {"v": 0, "s": 0, "p": 0, "g": 0}
    seen = {}
    nranks = len(T.cores)
    sends = rank < nranks - 1

    def need(q, *toks):
        best = {}
        for t in toks:
            if t is not None:
                best[t[0]] = max(best.get(t[0], 0), t[1])
        for s in sorted(best):
            if seen.get((q, s), 0) < best[s]:
                queue[q].wait_ge(T.sem[s], best[s])
                seen[(q, s)] = best[s]

    def done(q, ins):
        count[q] += 1
        ins.then_inc(T.sem["c" + q], 1)
        return ("c" + q, count[q])

    def dma(q, sem, out, in_, *deps):
        need(q, *deps)
        queue[q].dma_start(out, in_).then_inc(T.sem[sem], 16)
        return (sem, 16)

    def ts(out, in0, s1, s2, op0, op1, *deps):
        need("v", *deps)
        if op1 is None:
            return done("v", V.tensor_scalar(out, in0, s1, None, op0))
        return done("v", V.tensor_scalar(out, in0, s1, s2, op0, op1))

    def tt(out, a, b, op, *deps):
        need("v", *deps)
        return done("v", V.tensor_tensor(out, a, b, op))

    def vcopy(out, in_, *deps):
        need("v", *deps)
        return done("v", V.tensor_copy(out, in_))

    def fill(ap, c):
        return done("v", V.memset(ap, c))

    def act(out, in_, *deps):
        need("s", *deps)
        return done("s", S.activation(out, in_, ACT.Copy))

    def act2(out, in_, func, bias, scale, *deps):
        need("s", *deps)
        return done("s", S.activation(out, in_, func, bias=bias, scale=scale))

    def mm(out, lhsT, rhs, start, stop, *deps):
        need("p", *deps)
        return done("p", P.matmul(out, lhsT, rhs, start, stop))

    t_s = [dma("y", "ds0", T.sl_i[0:8, :], T.slot[:, 0:1536]), dma("s", "ds1", T.sl_i[8:16, :], T.slot[:, 1536:3072])]
    t_x = [dma("y", "dx0", T.xs[:, 0:1536], T.x[:, 0:1536]), dma("s", "dx1", T.xs[:, 1536:3072], T.x[:, 1536:3072])]
    t_w = dma("y", "dw", T.wc[:], T.w[:])

    f_one = fill(T.ones[:], 1.0)
    f_m2 = fill(T.m2[:], 0.0)
    f_m3 = fill(T.m3[:], float(UNIT))

    def sel(out, in_, pattern, op, base, cm, *deps):
        need("g", *deps)
        return done("g", g.affine_select(out, in_, pattern, op, 0.0, base, cm))

    c_wd = sel(T.wd[:], T.ones[0:16, :], [[-1, 288]], A.is_equal, 15, 16, f_one)
    c_id = sel(T.ident[:], T.ones[:, 0:128], [[-1, 128]], A.is_equal, 0, 1)
    t0 = sel(T.bt[:], T.ones[:, 0:128], [[-16, 8], [0, 16]], A.is_ge, 0, 1)
    c_b = sel(T.bm[:], T.bt[:], [[16, 8], [0, 16]], A.is_ge, 15, -1, t0)
    c_lm = sel(T.lm[:], T.bm[:], [[1, 128]], A.is_gt, 0, -1, c_b)
    c_m3 = sel(T.m3[:], T.m3[:], [[-1, 16], [-16, 8], [0, 16]], A.is_equal, 0, 1, f_m3)
    c_cio = done("g", g.iota(T.cio[:], [[1, NC]], 0, 0, allow_small_or_imprecise_dtypes=True))
    done("g", g.iota(T.pi[:], [[0, 1]], 0, 1))
    done("g", g.iota(T.ml[:], [[0, 2], [1, 16]], 0, 0, allow_small_or_imprecise_dtypes=True))
    c_io = done("g", g.iota(T.hi192[:], [[NC, 32]], 0, 0, allow_small_or_imprecise_dtypes=True))
    f_m2l = act(T.m2l[:], T.m2[:], f_m2)
    c_192 = act2(T.i192[:], T.ident[:], ACT.Silu, 0.0, 192.0, c_id)
    c_dg = None
    for i in range(ND - ND_S):
        c_dg = act2(T.dgm[:, 128 * i:128 * i + 128], T.ident[:], ACT.Copy, 0.0, -2.0 * (ND_S + i - MID), c_id)
    c_m2 = None
    for q in range(16):
        act(T.m2[:, 128 * q + q:128 * q + 128:16], T.bm[:, q:128:16], c_b, f_m2, f_m2l)
    for q in range(16):
        c_m2 = act(T.m2l[:, 128 * q + q:128 * q + 128:16], T.lm[:, q:128:16], c_lm, f_m2l)

    t_k = None
    for i in range(2):
        v0 = vcopy(T.sl_h[:, 768 * i:768 * i + 768], T.sl_i[:, 768 * i:768 * i + 768], *t_s)
        for h in range(2):
            for q in range(16):
                o, c = 128 * h + 15 - q, 96 * h + 48 * i
                t_k = mm(T.mis[:, c:c + 48], T.wd[:, o:o + 128], T.sl_h[:, 768 * i + q:768 * i + 768:16], q == 0, q == 15, v0, c_wd)
    f_zero = fill(T.zero[:], 0.0)
    fill(T.ct[:, 0:1], -128.0)
    fill(T.ct[:, F + 1:F + 16], 0.0)
    fill(T.oh[:, F:F + 16], 0.0)
    f_end = fill(T.srt[:, 0:8], NEG)
    for e in range(1, max(MID - ND_S, ND - 1 - MID) + 1):
        f_end = fill(T.e2r[:, 128 * e:128 * e + 128], float(e * e))

    def low(buf, *deps, c=int(NEG)):
        need("g", *deps)
        return done("g", g.iota(buf[:], [[0, S_TOK]], c, 0, allow_small_or_imprecise_dtypes=True))

    need("g", f_zero)
    g.dma_start(T.losb[:], T.zero[:]).then_inc(T.sem["dz"], 16)
    z_a = low(T.los, c=0)
    c_kc = done("g", g.iota(T.kc[:], [[HI, 32], [UNIT, 32]], int(SHIFT), 0, allow_small_or_imprecise_dtypes=True))

    st = {"lane": None, "wm": None, "mx": None, "za": z_a, "zb": ("dz", 16)}

    def off_chip_of(src):
        r = T.rank_of(src)
        return [d for d in T.cores[r + 1:] if d not in topo.cores_of(src)]

    def link(src, dst):
        eng = topo.engines(src, dst)
        offs = off_chip_of(src)
        if dst in offs:
            return eng
        if offs:
            eng = [e for e in eng if e not in topo.engines(src, offs[0])]
        return eng[::2]

    def arrivals(r):
        return len(link(T.cores[r], core))

    def nothing(*a):
        return None

    def sort_pass(nd, dig, off, dep, ps_free, early_v, inter, hook2, hook1, fillers, late):
        mm(T.acc[:, 256:256 + EV], T.i192[:], dig[:, 1:NC:2], True, False, dep, c_192)
        t_po = mm(T.acc[:, 256:256 + EV], T.ident[:], T.cio[:, 1:NC:2], False, True, c_id, c_cio)
        t_dl = act2(T.dl[:], dig, ACT.Copy, -float(MID), 1.0, dep)
        t_sq = act2(T.sq[:], dig, ACT.Square, -float(MID), 1.0, dep)
        v_oh, v_po = None, None
        for d in range(nd):
            if d == 4:
                early_v()
            if d == 12:
                v_po = vcopy(T.poff[:], T.acc[:, 256:256 + EV], t_po)
            v_oh = ts(T.oh[:, NC * d:NC * d + NC], dig, float(d), None, A.is_equal, None, dep)
        f_v, f_s = NC * nd, F - NC * nd
        n = f_s // 512 + (f_s % 512 > 0)
        relu, s_oh = list(ps_free), None
        for b in range(n):
            o, w, c, t = 512 * (b % 3), min(512, f_s - 512 * b), 512 * b, None
            while c < 512 * b + w:
                i = c // NC
                m = min(NC * (i + 1), 512 * b + w)
                e, j = nd + i - MID, nd + i - ND_S
                z, k = T.psa[:, o + c - 512 * b:o + m - 512 * b], c - NC * i
                if e:
                    mm(z, T.dgm[:, 128 * j:128 * j + 128], T.dl[:, k:k + m - c], True, False, t_dl, c_dg, relu[b % 3])
                    mm(z, T.e2r[:, 128 * abs(e):128 * abs(e) + 128], T.ones[0:1, 0:m - c], False, False, f_end)
                t = mm(z, T.ident[:], T.sq[:, k:k + m - c], e == 0, True, t_sq, c_id, relu[b % 3])
                c = m
            if b == n - 1:
                inter()
            s_oh = act2(T.oh[:, f_v + 512 * b:f_v + 512 * b + w], T.psa[:, o:o + w], ACT.Relu, 1.0, -1.0, t, f_end)
            relu[b % 3] = s_oh
        sc, c, tok = None, 0, {}
        while c < F:
            w = min(3072, (f_v if c < f_v else F) - c)
            need("v", v_oh, sc, s_oh if c >= f_v else None)
            init = -128.0 if c == 0 else T.ct[:, c:c + 1]
            sc = done("v", V.tensor_tensor_scan(T.ct[:, c + 1:c + w + 1], T.oh[:, c:c + w], T.zero[:, 0:w], init, A.add, A.add))
            c += w
            tok[c] = sc
        bank = list(relu)

        def early(b):
            z, a = T.psa[:, 512 * (b % 3):512 * (b % 3) + 512], 1024 * b
            mm(z, T.lm[:], T.oh[:, a:a + 1024:2], True, False, v_oh, s_oh if a + 1024 > f_v else None, c_lm, bank[b % 3])

        for b in range(3):
            early(b)
        hook2()
        need("s", v_oh, s_oh, v_po)
        s_2 = done("s", S.activation(T.g2[:], T.oh[:].indirect(T.poff[:]), ACT.Copy))
        need("s", sc)
        s_1 = done("s", S.activation(T.g1[:], T.ct[:].indirect(T.poff[:]), ACT.Copy))
        hook1()
        red, d, t = [], 0, None
        for b in range(6):
            z, a = T.psa[:, 512 * (b % 3):512 * (b % 3) + 512], 1024 * b
            if b > 2:
                early(b)
            t = tok[min(k for k in tok if k >= a + 1024)]
            t = mm(z, T.bm[:], T.ct[:, a:a + 1024:2], False, True, t, c_b)
            bank[b % 3] = tt(T.msk[:, 512 * b:512 * b + 512], z, T.oh[:, a:a + 1024:2], A.mult, t)
            red.append(bank[b % 3])
            if b == 2:
                fillers(sc)
                for q in range(16):
                    mm(T.mis[:, 256:256 + EV], T.m2l[:, 128 * q:128 * q + 128], T.g2[:, q:16 * EV:16], q == 0, False, s_2, c_m2)
            if b in (2, 4, 5):
                while EV * (d + 1) <= 512 * (b - 1):
                    mm(T.acc[:, 0:EV], T.ident[:], T.msk[:, EV * d:EV * d + EV], d == 0, False, red[b - 2])
                    d += 1
        t_o = None
        for q in range(16):
            t_o = mm(T.mis[:, 256:256 + EV], T.m2[:, 128 * q:128 * q + 128], T.g1[:, q:16 * EV:16], False, q == 15, s_1)
        while d < ND:
            t = mm(T.acc[:, 0:EV], T.ident[:], T.msk[:, EV * d:EV * d + EV], False, d == ND - 1, red[min(5, (EV * d + EV - 1) // 512)])
            d += 1
        late()
        ts(off[:, 1:NC:2], T.mis[:, 256:256 + EV], 2048.0, None, A.add, None, t_o)
        return ts(off[:, 0:NC:2], T.acc[:, 0:EV], 2048.0, None, A.add, None, t), sc, bank

    def layer(li, src, src_toks, key_tok, out, piece_done):
        v = vcopy(T.ki[:], T.mis[:, 0:NC], key_tok)
        v_lo = ts(T.loi[:], T.ki[:], 31, None, A.bitwise_and, None, v)
        v_d1 = vcopy(T.dig1[:], T.loi[:], v_lo)
        kt, t_p, jt, pb, ko = {}, [], [None], [], []

        def pack_keys():
            a = ts(T.keyi[:], T.ki[:], 1023, None, A.bitwise_and, None, v)
            b = ts(T.h16[:], T.ki[:], 992, None, A.bitwise_and, None, v)
            kt["pk"] = tt(T.pk[:], T.keyi[:], T.h16[:], A.add, a, b)
            kt["key"] = a

        def row_bank(ps, b, c, with_src, *deps):
            t = None
            if with_src:
                mm(ps[:, 512 * b:512 * b + 512], T.ident[:], src[:, c:c + 512], True, False, c_id, *(deps + tuple(src_toks)))
            for q in range(16):
                t = mm(ps[:, 512 * b + q:512 * b + 512:16], T.m3[:, 128 * q:128 * q + 128], T.pk[:, c // 16:c // 16 + 32],
                       not with_src, q == 15 or not with_src, kt["pk"], c_m3, *deps)
            return t

        def pack_p(i, free):
            pb.append(row_bank(T.psb, i % 3, 512 * i, True, free))

        def pack_s(i):
            t_p.append(act2(T.packed[:, 512 * i:512 * i + 512], T.psb[:, 512 * (i % 3):512 * (i % 3) + 512], ACT.Copy, SHIFT, 1.0,
                            pb[i], st["mx"]))

        def packs_x():
            for i in range(3):
                pack_p(i, None)

        def packs_y():
            for i in range(3):
                pack_s(i)
            pack_p(3, t_p[0])

        def packs_z():
            pack_s(3)

        def packs_l():
            for i in (4, 5):
                pack_p(i, t_p[i - 3])
                pack_s(i)

        def fillers(sc):
            if sends:
                jt[0] = mm(T.mis[:, 0:32], T.bm[:], T.ct[:, NC:F + 1:NC], True, True, sc)
            ko.append(vcopy(T.koff[:], T.keyi[:], kt["key"]))
            if st["lane"] is None:
                a = ts(T.li[:], T.pi[:], 15, None, A.bitwise_and, None, c_io)
                a = vcopy(T.lane[:], T.li[:], a)
                st["lane"] = ts(T.dq[:], T.ml[:], T.lane[:], None, A.is_equal, None, a)

        g_b = low(T.pkb, st["mx"])
        v_o1, _, psa_t = sort_pass(ND_V[0], T.dig1[:], T.off1, v_d1, [None] * 3, pack_keys, packs_x, packs_y, packs_z, fillers,
                                   packs_l)
        need("v", v_o1, st["za"], *t_p[:(16 * SP_V + 511) // 512])
        v_s1 = done("v", V.tensor_copy(T.los[:].indirect(T.off1[:, 0:SP_V]), T.packed[:, 0:16 * SP_V]))
        need("s", v_o1, st["zb"], *t_p)
        s_s1 = done("s", S.activation(T.losb[:].indirect(T.off1[:, SP_V:NC]), T.packed[:, 16 * SP_V:], ACT.Silu))
        pk_r = [None, None]

        def key_mm(h, *deps):
            for b in range(3):
                pk_r[h] = row_bank((T.psa, T.psb)[h], b, 1536 * h + 512 * b, False, *deps)

        def key_rows(h):
            return act2(T.krow[:, 1536 * h:1536 * h + 1536], (T.psa, T.psb)[h][:], ACT.Copy, SHIFT, 1.0, pk_r[h])

        key_mm(1, *t_p[3:6])
        t_hi, v_j, sc_hi = None, None, 1.0 / (16.0 * HI)
        if sends:
            v_j = ts(T.ji[:], T.mis[:, 0:32], 2048.0, None, A.add, None, jt[0], v_o1)
        need("v", v_s1)
        need("s", s_s1)
        t_da = ("da%d" % li, 16)
        for c in range(S_TOK - PC, -1, -PC):
            e_a = ts(T.ext[:, c:c + PC], T.los[:, c:c + PC], sc_hi, None, A.mult, None)
            e_b = act2(T.yo[:, c:c + PC], T.losb[:, c:c + PC], ACT.Copy, 0.0, sc_hi)
            if c <= 16 * SC_V < c + PC:
                need("g", e_a, s_s1)
                g.dma_start(T.los[:, 16 * SC_V:], T.losb[:, 16 * SC_V:], accum_op=A.add).then_inc(T.sem[t_da[0]], 16)
            for last, x, t in ((False, T.ext, e_a), (True, T.yo, e_b)):
                for q in range(16):
                    t_hi = mm(T.mis[:, c // 16:(c + PC) // 16], T.m2[:, 128 * q:128 * q + 128], x[:, c + q:c + PC:16],
                              q == 0 and not last, q == 15 and last, t, c_m2, v_j)
        g_a = low(T.packed, v_s1, s_s1)
        t_kr = [None, None]
        t_mk = None
        if sends:
            v_q = ts(T.jq[:], T.ji[:], 15, None, A.bitwise_and, None, v_j)
            v_c = ts(T.jc[:], T.ji[:], 4, None, A.logical_shift_right, None, v_j)
            t_mk = ts(T.mkt[:], T.jq[:], T.lane[:], None, A.is_gt, None, v_q, st["lane"])
            v = tt(T.jt[:], T.jc[:], T.dq[:], A.mult, v_c, st["lane"])
            need("v", v)
            for b in range(2):
                v = done("v", V.tensor_reduce(T.cw[:, b:b + 1], T.jt[:, 16 * b:16 * b + 16], AxisListType.X, A.add))
        v_d2 = ts(T.dig2[:], T.mis[:, 0:NC], MAGIC, MAGIC + 1.0, A.add, A.subtract, t_hi)

        def lists(sc):
            if sends:
                for b in range(2):
                    kt["l"] = ts(T.lst[:, b:64:2], T.hi192[:], T.cw[:, b:b + 1], None, A.add, None, v, c_io)

        v_o2, v_ct, _ = sort_pass(ND_V[1], T.dig2[:], T.off2, v_d2, [None] * 3, nothing, nothing, nothing, nothing, lists, nothing)
        t_e, p, ps_a = None, None, v_o2
        if sends:
            need("s", kt["l"], v_ct)
            s_1 = done("s", S.activation(T.e1[:], T.ct[:].indirect(T.lst[:]), ACT.Copy))
            s_2 = done("s", S.activation(T.e2[:], T.oh[:].indirect(T.lst[:]), ACT.Copy))
            for q in range(16):
                mm(T.mis[:, 0:64], T.m2[:, 128 * q:128 * q + 128], T.e1[:, q:1024:16], q == 0, False, s_1, v_o2)
            for b in range(2):
                mm(T.psa[:, 512 * b:512 * b + 512], T.ident[:], T.e2[:, 512 * b:512 * b + 512], True, False, s_2, v_o2)
                for i in range(16):
                    c = 512 * b + 32 * i
                    p = mm(T.psa[:, c:c + 32], T.ident[:], T.mkt[:], False, i == 15, t_mk)
        need("v", v_o2, g_a, v_s1, s_s1)
        v = done("v", V.tensor_tensor(T.packed[:].indirect(T.off2[:, 0:SC_V]), T.los[:, 0:16 * SC_V], T.losb[:, 0:16 * SC_V], A.add))
        need("s", v_o2, g_b, t_da)
        s_w = done("s", S.activation(T.pkb[:].indirect(T.off2[:, SC_V:NC]), T.los[:, 16 * SC_V:], ACT.Silu))
        if sends:
            s_3 = ps_a = act2(T.e3[:], T.psa[:, 0:1024], ACT.Relu, -1.0, 1.0, p)
            for q in range(16):
                t_e = mm(T.mis[:, 0:64], T.m2[:, 128 * q:128 * q + 128], T.e3[:, q:1024:16], False, q == 15, s_3)
        key_mm(0, ps_a)
        t_kr[1] = key_rows(1)
        need("v", v, s_w)
        v_mx = done("v", V.tensor_tensor_scan(T.srt[:, 8:], T.packed[:], T.pkb[:], NEG, A.max, A.max))
        st["mx"] = v_mx
        tl = T["tl%d" % li]
        if sends:
            v_e = ts(T.eoff[:], T.mis[:, 0:64], 2055.0, None, A.add, None, t_e)
            v_t = tt(tl[:], T.srt[:].indirect(T.eoff[:]), T.kc[:], A.subtract, v_mx, v_e, c_kc)
            need("g", v_t)
            off_chip = off_chip_of(core)
            on_chip = [d for d in T.cores[rank + 1:] if d not in off_chip]
            total = 0
            for group in [c for c in (off_chip[:1], on_chip + off_chip[1:]) if c]:
                trans = []
                for d in group:
                    eng = link(core, d)
                    total += len(eng)
                    rid, pid = topo.addr(d, core)
                    trans.append(RemoteDMATransfer(dst_ids=[DstId(rid=rid, pnc=pid)], dma_engine_mask=mask_of(eng),
                                                   remote_sem=T.sem["r%d%d" % (li, rank)], srcs=[tl[:]],
                                                   dsts=[T["ld%d%d" % (li, rank)][:]]))
                g.remote_dma_fused(trans, local_sem=T.sem["lo%d" % li])
            st["lo%d" % li] = total
        if li == 0:
            st["zb"] = low(T.losb, v_mx, c=0)
        a = 64 if sends else 96
        need("v", v_mx)
        v_a = done("v", V.tensor_copy(T.los[:, 0:16 * a], T.srt[:, 8:].indirect(T.off2[:, 0:a])))
        need("s", v_mx)
        s_a = done("s", S.activation(T.los[:, 16 * a:], T.srt[:, 8:].indirect(T.off2[:, a:NC]), ACT.Copy))
        t_kr[0] = key_rows(0)
        if st["wm"] is None:
            st["wm"] = act2(T.wm[:], T.m2[:], ACT.Copy, 0.0, T.wc[:], c_m2, t_w)
        dst = T.yl if rank > 0 else out
        ys = []
        for c, e in ((CUT, S_TOK), (0, CUT)):
            need("v", v_a, s_a, t_kr[1], t_kr[0] if c < 1536 else None)
            ys.append(done("v", V.tensor_tensor(dst[:, c:e], T.los[:].indirect(T.off1[:, c // 16:e // 16]), T.krow[:, c:e], A.subtract)))
            if rank == 0:
                for i, j in ((CUT, STORE), (STORE, S_TOK)) if c else ((0, CUT),):
                    piece_done(i, j, ys[-1])
        if li == 0:
            st["za"] = low(T.los, *ys, c=0)
        if rank > 0:
            parts, c = [], CUT
            for ps, o in ((T.acc, 0), (T.psa, 1024), (T.psb, 1024)):
                n = min(512, S_TOK - c)
                t = mm(ps[:, o:o + n], T.ident[:], T.yl[:, c:c + n], True, True, ys[0], t_kr[0], t_kr[1])
                parts.append((ps, o, c, n, t))
                c += n
            tin = T["ld%d0" % li]
            v_in = ("r%d0" % li, arrivals(0))
            merge = []
            for r in range(1, rank):
                ps = (T.psa, T.psb)[r % 2]
                for b in range(2):
                    t = mm(ps[:, 512 * b:512 * b + 512], T.ident[:], T["ld%d%d" % (li, r)][:, 512 * b:512 * b + 512], True, True,
                           ("r%d%d" % (li, r), arrivals(r)), ps_a, t_kr[0])
                merge.append(((T.ta, T.tb)[r % 2], ps, t))
            for nxt, ps, t in merge:
                v_in = tt(nxt[:], ps[:, 0:1024], tin[:], A.max, t, v_in)
                tin = nxt
            need("s", v_in, ko[0])
            s_t = done("s", S.activation(T.ext[:, CUT:], tin[:].indirect(T.koff[:, CUT // 16:]), ACT.Copy))
            piece_done(0, CUT, tt(out[:, 0:CUT], tin[:].indirect(T.koff[:, 0:CUT // 16]), T.yl[:, 0:CUT], A.max, v_in, ys[1], ko[0]))
            for ps, o, c, n, t in parts:
                v = tt(out[:, c:c + n], ps[:, o:o + n], T.ext[:, c:c + n], A.max, t, s_t)
                if c + n == STORE:
                    piece_done(CUT, STORE, v)
            piece_done(STORE, S_TOK, v)

    hk = []

    def hash_piece(c, e, tok):
        t = None
        for q in range(16):
            t = mm(T.mis[:, c // 16:e // 16], T.wm[:, 128 * q:128 * q + 128], T.y1[:, c + q:e:16], q == 0, q == 15, tok, st["wm"])
        hk.append((tok, t))

    def store_piece(c, e, tok):
        dma("y", {0: "dy0", CUT: "dy1"}.get(c, "dy2"), T.y[:, c:e], T.yo[:, c:e], tok)

    layer(0, T.xs, t_x, t_k, T.y1, hash_piece)
    layer(1, T.y1, [h[0] for h in hk], max(h[1] for h in hk), T.yo, store_piece)

    for q in ("v", "s", "p", "g"):
        need("g", ("c" + q, count[q]))
    for s in ("ds0", "ds1", "dx0", "dx1", "dw", "dz", "da0", "da1", "dy0", "dy1", "dy2"):
        need("g", (s, 16))
    if sends:
        for li in range(2):
            need("g", ("lo%d" % li, st["lo%d" % li]))
